import numpy as np
import ml_dtypes


def mxq(x, axis, fmt="e4m3"):
    dtype, down = {"e4m3": (ml_dtypes.float8_e4m3fn, 7), "e5m2": (ml_dtypes.float8_e5m2, 14)}[fmt]
    v = np.moveaxis(np.asarray(x, np.float32).astype(ml_dtypes.bfloat16).astype(np.float64), axis, -1)
    blocks = v.reshape(v.shape[:-1] + (-1, 32))
    amax = np.abs(blocks).max(-1, keepdims=True)
    byte = np.maximum(np.where(amax > 0, np.frexp(amax)[1] - 1 + 127, 0) - down, 1)
    scale = np.exp2(byte - 127.0)
    codes = (blocks / scale).astype(np.float32).astype(dtype).astype(np.float64)
    return np.moveaxis((codes * scale).reshape(v.shape), -1, axis)


WIDE = False


def mx_kscale(k):
    if not WIDE:
        return np.ones(k)
    levels = np.array([10, -10, 5, -5, 0])
    if k % 512:
        return np.exp2(np.random.permutation(np.resize(levels, k // 32))).repeat(32)
    a = np.empty((k // 512, 16))
    for p in range(k // 512):
        a[p, :8] = np.random.permutation(np.resize(levels, 8))
        for g in range(8):
            far = levels[np.abs(levels - a[p, g]) >= 10]
            a[p, g + 8] = far[np.random.randint(len(far))]
    return np.exp2(a.ravel()).repeat(32)


def f64(x):
    return np.asarray(x).astype(np.float64)


def striped(idx):
    return np.tile(idx.reshape(-1, 16).T, (8, 1)).astype(np.uint16)


def unstriped(offs):
    return offs[:16].T.reshape(-1).astype(np.int64)


def pack_weight(w):
    k, n = w.shape
    w = f64(np.asarray(w, np.float32).astype(ml_dtypes.bfloat16)).reshape(k // 32, 32, n)
    amax = np.abs(w).max(1)
    byte = np.clip(np.where(amax > 0, np.frexp(amax)[1] - 1 + 127 - 7, 1), 1, 254)
    scaled = (w * np.exp2(127.0 - byte)[:, None, :]).reshape(k, n).astype(np.float32)
    words = np.ascontiguousarray(scaled.reshape(k // 512, 128, 4, n).transpose(0, 1, 3, 2)).astype(ml_dtypes.float8_e4m3fn).view(np.uint8)
    return words, np.ascontiguousarray(byte.astype(np.uint8).reshape(k // 512, 16, n))


def unpack_weight(words, scales):
    g, p, n, _ = words.shape
    vals = np.ascontiguousarray(words).view(ml_dtypes.float8_e4m3fn).astype(np.float64) * np.repeat(np.exp2(scales.astype(np.float64) - 127.0), 8, axis=1)[..., None]
    return vals.transpose(0, 1, 3, 2).reshape(g * 512, n)


K, T, S, V, N, U = 1024, 2048, 1536, 512, 128, 1024


def setup_inputs():
    n = np.random.standard_normal
    s = mx_kscale(K)[:, None]
    packed_xT = pack_weight(n((K, T)) * s)
    return {
        "x_words": packed_xT[0],
        "x_scales": packed_xT[1],
        "w1": (n((K, N)) / np.sqrt(3 * K) / s).astype(np.float32),
        "w2": (n((K, N)) / np.sqrt(3 * K) / s).astype(np.float32),
        "w3": (n((K, N)) / np.sqrt(3 * K) / s).astype(np.float32),
        "offs": striped(np.random.permutation(T)[:S]),
        "to1": striped(np.random.permutation(U)[:V]),
        "to2": striped(np.random.permutation(U)[:V]),
        "to3": striped(np.random.permutation(U)[:V]),
    }


def reference(x_words, x_scales, w1, w2, w3, offs, to1, to2, to3):
    xq = unpack_weight(x_words, x_scales)[:, unstriped(offs)]
    o0 = np.zeros((N, U))
    o0[:, unstriped(to1)] = mxq(f64(w1), 0, "e4m3").T @ xq[:, :V]
    o1 = np.zeros((N, U))
    o1[:, unstriped(to2)] = mxq(f64(w2), 0, "e4m3").T @ xq[:, V:2 * V]
    o2 = np.zeros((N, U))
    o2[:, unstriped(to3)] = mxq(f64(w3), 0, "e4m3").T @ xq[:, 2 * V:3 * V]
    return o0 + o1 + o2

@@ -1,0 +1,120 @@
+from contextlib import ExitStack
+
+import concourse.mybir as mybir
+from concourse.masks import make_identity
+
+K, T, S, V, N, U = 1024, 2048, 1536, 512, 128, 1024
+TAPS = 3
+P = 128
+PACK = 4
+PASSES = K // (P * PACK)
+BANK = 512
+FLOPS = 2 * K * N * S
+
+F32 = mybir.dt.float32
+BF16 = mybir.dt.bfloat16
+I32 = mybir.dt.int32
+U32 = mybir.dt.uint32
+U16 = mybir.dt.uint16
+U8 = mybir.dt.uint8
+FP8X4 = mybir.dt.float8_e4m3fn_x4
+
+
+def tile_picked_spconv_none_p_kernel(tc, x_words, x_scales, w1, w2, w3, offs, to1, to2, to3, out):
+    nc = tc.nc
+    weights = (w1, w2, w3)
+    with ExitStack() as ctx:
+        keep = ctx.enter_context(tc.tile_pool(name="keep", bufs=1))
+        stage = ctx.enter_context(tc.tile_pool(name="stage", bufs=2))
+        psum = ctx.enter_context(tc.psum_pool(name="psum", bufs=1))
+
+        picks = keep.tile([P, S // 16], U16, name="picks")
+        maps = [keep.tile([P, V // 16], U16, name=f"map{d}") for d in range(TAPS)]
+        scale_table = keep.tile([P, T], U8, name="scale_table", align_bytes=64)
+        word_tables = [keep.tile([P, T], I32, name=f"word_table{z}", align_bytes=64) for z in range(PASSES)]
+        raw = [keep.tile([P, PASSES, PACK, N], F32, name=f"raw{d}") for d in range(TAPS)]
+
+        nc.vector.memset(scale_table[:].bitcast(I32), 0)
+        nc.sync.dma_start(picks[:], offs)
+        for q in range(4):
+            nc.sync.dma_start(scale_table[32 * q : 32 * q + 8, :].bitcast(I32), x_scales[:, 4 * q : 4 * q + 4, :].bitcast(I32))
+
+        def load_words(z):
+            nc.sync.dma_start(word_tables[z][:], x_words[z].rearrange("p c r -> p (c r)").bitcast(I32))
+
+        def load_weight(d):
+            nc.sync.dma_start(raw[d][:].rearrange("p z j m -> p z (j m)"), weights[d].rearrange("(z p j) m -> p z (j m)", z=PASSES, j=PACK))
+
+        load_words(0)
+        load_weight(0)
+        load_weight(1)
+        load_words(1)
+        load_weight(2)
+        for tile, dram in zip(maps, (to1, to2, to3)):
+            nc.sync.dma_start(tile[:], dram)
+
+        placed = [keep.tile([P, U], F32, name=f"placed{d}") for d in range(TAPS)]
+        for d in range(TAPS):
+            nc.vector.memset(placed[d][:], 0.0)
+        ident = keep.tile([P, P], F32, name="ident")
+        nc.vector.memset(ident[:], 0.0)
+        make_identity(nc, ident[:], nomemset=True)
+
+        x_scale = keep.tile([P, S], U8, name="x_scale", align_bytes=64)
+        nc.vector.tensor_copy(x_scale[:], scale_table[:].indirect(picks[:]))
+        x_first = keep.tile([P, S], U32, name="x_first", align_bytes=64)
+        nc.vector.tensor_copy(x_first[:], word_tables[0][:].bitcast(U32).indirect(picks[:]))
+
+        w_codes, w_scale = [], []
+        for d in range(TAPS):
+            grouped = stage.tile([P, PASSES, N, PACK], BF16, name="grouped", tag="stage", align_bytes=64)
+            nc.scalar.copy(grouped[:], raw[d][:].rearrange("p z j m -> p z m j"))
+            codes = keep.tile([P, PASSES * N], U32, name=f"w_codes{d}", align_bytes=64)
+            scale = keep.tile([P, PASSES * N], U8, name=f"w_scale{d}", align_bytes=64)
+            nc.vector.quantize_mx(out=codes[:].bitcast(FP8X4), scales=scale[:], in_=grouped[:].rearrange("p z m j -> p (z m j)"))
+            w_codes.append(codes)
+            w_scale.append(scale)
+
+        for d in range(TAPS):
+            x_second = keep.tile([P, V], U32, name=f"x_second{d}", align_bytes=64)
+            nc.vector.tensor_copy(x_second[:], word_tables[1][:].bitcast(U32).indirect(picks[:, d * V // 16 : (d + 1) * V // 16]))
+            cols = slice(d * V, (d + 1) * V)
+            acc = psum.tile([P, V], F32, name=f"acc{d}")
+            for z, codes in enumerate((x_first[:, cols], x_second[:])):
+                nc.tensor.matmul_mx(
+                    out=acc[:],
+                    lhsT=w_codes[d][:, z * N : (z + 1) * N].bitcast(FP8X4),
+                    lhsT_scale=w_scale[d][:, z * N : (z + 1) * N],
+                    rhs=codes.bitcast(FP8X4),
+                    rhs_scale=x_scale[4 * z : P, cols],
+                    start=(z == 0),
+                    stop=(z == PASSES - 1),
+                )
+            y = stage.tile([P, V], F32, name="y", tag="stage", align_bytes=64)
+            nc.scalar.copy(y[:], acc[:])
+            nc.vector.tensor_copy(placed[d][:].indirect(maps[d][:]), y[:])
+
+        blocks = BANK // P
+        for h in range(U // BANK):
+            turned = psum.tile([P, BANK], F32, name=f"turned{h}")
+            for d in range(2):
+                for b in range(blocks):
+                    nc.tensor.matmul(
+                        turned[:, b * P : (b + 1) * P],
+                        placed[d][:, h * BANK + b * P : h * BANK + (b + 1) * P],
+                        ident[:],
+                        start=(d == 0 and b == 0),
+                        stop=(d == 1 and b == blocks - 1),
+                        is_transpose=True,
+                    )
+            pair_t = keep.tile([P, BANK], F32, name=f"pair_t{h}")
+            nc.scalar.copy(pair_t[:], turned[:])
+            pair = psum.tile([P, BANK], F32, name=f"pair{h}")
+            for b in range(blocks):
+                nc.tensor.transpose(pair[:, b * P : (b + 1) * P], pair_t[:, b * P : (b + 1) * P], ident[:])
+            for c in range(2):
+                w = BANK // 2
+                total = keep.tile([P, w], F32, name=f"total{h}{c}")
+                nc.vector.tensor_tensor(total[:], pair[:, c * w : (c + 1) * w], placed[2][:, h * BANK + c * w : h * BANK + (c + 1) * w], mybir.AluOpType.add)
+                queue = nc.sync if c == 0 else nc.scalar
+                queue.dma_start(out[:, h * BANK + c * w : h * BANK + (c + 1) * w], total[:])

@@ -25,49 +25,59 @@ def tile_picked_spconv_none_p_kernel(tc, x_words, x_scales, w1, w2, w3, offs, to
     weights = (w1, w2, w3)
     with ExitStack() as ctx:
         keep = ctx.enter_context(tc.tile_pool(name="keep", bufs=1))
-        stage = ctx.enter_context(tc.tile_pool(name="stage", bufs=2))
         psum = ctx.enter_context(tc.psum_pool(name="psum", bufs=1))
 
         picks = keep.tile([P, S // 16], U16, name="picks")
         maps = [keep.tile([P, V // 16], U16, name=f"map{d}") for d in range(TAPS)]
         scale_table = keep.tile([P, T], U8, name="scale_table", align_bytes=64)
         word_tables = [keep.tile([P, T], I32, name=f"word_table{z}", align_bytes=64) for z in range(PASSES)]
-        raw = [keep.tile([P, PASSES, PACK, N], F32, name=f"raw{d}") for d in range(TAPS)]
+        raw = {}
 
-        nc.vector.memset(scale_table[:].bitcast(I32), 0)
         nc.sync.dma_start(picks[:], offs)
-        for q in range(4):
-            nc.sync.dma_start(scale_table[32 * q : 32 * q + 8, :].bitcast(I32), x_scales[:, 4 * q : 4 * q + 4, :].bitcast(I32))
+        nc.sync.dma_start(scale_table[0:32, :].bitcast(I32), x_scales.rearrange("z q c -> (z q) c").bitcast(I32))
+        nc.vector.memset(scale_table[32:64, :].bitcast(I32), 0)
+        nc.vector.memset(scale_table[64:128, :].bitcast(I32), 0)
 
         def load_words(z):
             nc.sync.dma_start(word_tables[z][:], x_words[z].rearrange("p c r -> p (c r)").bitcast(I32))
 
         def load_weight(d):
+            raw[d] = keep.tile([P, PASSES, PACK, N], F32, name=f"raw{d}", tag=f"shared{d % 2}", align_bytes=64)
             nc.sync.dma_start(raw[d][:].rearrange("p z j m -> p z (j m)"), weights[d].rearrange("(z p j) m -> p z (j m)", z=PASSES, j=PACK))
 
+        for tile, dram in zip(maps, (to1, to2, to3)):
+            nc.sync.dma_start(tile[:], dram)
         load_words(0)
         load_weight(0)
         load_weight(1)
         load_words(1)
-        load_weight(2)
-        for tile, dram in zip(maps, (to1, to2, to3)):
-            nc.sync.dma_start(tile[:], dram)
 
         placed = [keep.tile([P, U], F32, name=f"placed{d}") for d in range(TAPS)]
+        x_scale = keep.tile([P, S], U8, name="x_scale", align_bytes=64)
+        nc.vector.memset(x_scale[:].bitcast(I32), 0)
+        zero = keep.tile([P, 1], F32, name="zero")
+        nc.vector.memset(zero[:], 0.0)
         for d in range(TAPS):
-            nc.vector.memset(placed[d][:], 0.0)
+            nc.scalar.copy(placed[d][:], zero[:].to_broadcast([P, U]))
         ident = keep.tile([P, P], F32, name="ident")
         nc.vector.memset(ident[:], 0.0)
         make_identity(nc, ident[:], nomemset=True)
 
-        x_scale = keep.tile([P, S], U8, name="x_scale", align_bytes=64)
-        nc.vector.tensor_copy(x_scale[:], scale_table[:].indirect(picks[:]))
+        picked_rows = keep.tile([P, S], U8, name="picked_rows", align_bytes=64)
+        nc.vector.tensor_copy(picked_rows[:], scale_table[:].indirect(picks[:]))
+        for z in range(PASSES):
+            for q in range(4):
+                src = 16 * z + 4 * q
+                dst = 32 * q + 4 * z
+                nc.sync.dma_start(x_scale[dst : dst + 4, :].bitcast(I32), picked_rows[src : src + 4, :].bitcast(I32))
         x_first = keep.tile([P, S], U32, name="x_first", align_bytes=64)
         nc.vector.tensor_copy(x_first[:], word_tables[0][:].bitcast(U32).indirect(picks[:]))
 
         w_codes, w_scale = [], []
         for d in range(TAPS):
-            grouped = stage.tile([P, PASSES, N, PACK], BF16, name="grouped", tag="stage", align_bytes=64)
+            if d == 2:
+                load_weight(d)
+            grouped = keep.tile([P, PASSES, N, PACK], BF16, name=f"grouped{d}", align_bytes=64)
             nc.scalar.copy(grouped[:], raw[d][:].rearrange("p z j m -> p z m j"))
             codes = keep.tile([P, PASSES * N], U32, name=f"w_codes{d}", align_bytes=64)
             scale = keep.tile([P, PASSES * N], U8, name=f"w_scale{d}", align_bytes=64)
@@ -90,7 +100,7 @@ def tile_picked_spconv_none_p_kernel(tc, x_words, x_scales, w1, w2, w3, offs, to
                     start=(z == 0),
                     stop=(z == PASSES - 1),
                 )
-            y = stage.tile([P, V], F32, name="y", tag="stage", align_bytes=64)
+            y = keep.tile([P, V], F32, name=f"y{d}", tag="shared0" if d == 1 else f"y{d}", align_bytes=64)
             nc.scalar.copy(y[:], acc[:])
             nc.vector.tensor_copy(placed[d][:].indirect(maps[d][:]), y[:])
 

@@ -9,6 +9,7 @@ P = 128
 PACK = 4
 PASSES = K // (P * PACK)
 BANK = 512
+ROW0 = P - 16 * PASSES
 FLOPS = 2 * K * N * S
 
 F32 = mybir.dt.float32
@@ -31,25 +32,23 @@ def tile_picked_spconv_none_p_kernel(tc, x_words, x_scales, w1, w2, w3, offs, to
         maps = [keep.tile([P, V // 16], U16, name=f"map{d}") for d in range(TAPS)]
         scale_table = keep.tile([P, T], U8, name="scale_table", align_bytes=64)
         word_tables = [keep.tile([P, T], I32, name=f"word_table{z}", align_bytes=64) for z in range(PASSES)]
-        raw = {}
 
         nc.sync.dma_start(picks[:], offs)
-        nc.sync.dma_start(scale_table[0:32, :].bitcast(I32), x_scales.rearrange("z q c -> (z q) c").bitcast(I32))
-        nc.vector.memset(scale_table[32:64, :].bitcast(I32), 0)
-        nc.vector.memset(scale_table[64:128, :].bitcast(I32), 0)
+        nc.scalar.dma_start(scale_table[ROW0:P, :].bitcast(I32), x_scales.rearrange("z q c -> (z q) c").bitcast(I32))
+        nc.vector.memset(scale_table[0:ROW0, :].bitcast(I32), 0)
 
         def load_words(z):
             nc.sync.dma_start(word_tables[z][:], x_words[z].rearrange("p c r -> p (c r)").bitcast(I32))
 
-        def load_weight(d):
-            raw[d] = keep.tile([P, PASSES, PACK, N], F32, name=f"raw{d}", tag=f"shared{d % 2}", align_bytes=64)
-            nc.sync.dma_start(raw[d][:].rearrange("p z j m -> p z (j m)"), weights[d].rearrange("(z p j) m -> p z (j m)", z=PASSES, j=PACK))
+        def load_weight(d, tag):
+            raw = keep.tile([P, PASSES, PACK, N], F32, name=f"raw{d}", tag=tag, align_bytes=64)
+            nc.sync.dma_start(raw[:].rearrange("p z j m -> p z (j m)"), weights[d].rearrange("(z p j) m -> p z (j m)", z=PASSES, j=PACK))
+            return raw
 
         for tile, dram in zip(maps, (to1, to2, to3)):
             nc.sync.dma_start(tile[:], dram)
         load_words(0)
-        load_weight(0)
-        load_weight(1)
+        early = [load_weight(d, f"raw{d}") for d in range(2)]
         load_words(1)
 
         placed = [keep.tile([P, U], F32, name=f"placed{d}") for d in range(TAPS)]
@@ -67,40 +66,46 @@ def tile_picked_spconv_none_p_kernel(tc, x_words, x_scales, w1, w2, w3, offs, to
         nc.vector.tensor_copy(picked_rows[:], scale_table[:].indirect(picks[:]))
         for z in range(PASSES):
             for q in range(4):
-                src = 16 * z + 4 * q
+                src = ROW0 + 16 * z + 4 * q
                 dst = 32 * q + 4 * z
                 nc.sync.dma_start(x_scale[dst : dst + 4, :].bitcast(I32), picked_rows[src : src + 4, :].bitcast(I32))
         x_first = keep.tile([P, S], U32, name="x_first", align_bytes=64)
         nc.vector.tensor_copy(x_first[:], word_tables[0][:].bitcast(U32).indirect(picks[:]))
 
-        w_codes, w_scale = [], []
-        for d in range(TAPS):
-            if d == 2:
-                load_weight(d)
-            grouped = keep.tile([P, PASSES, N, PACK], BF16, name=f"grouped{d}", align_bytes=64)
-            nc.scalar.copy(grouped[:], raw[d][:].rearrange("p z j m -> p z m j"))
-            codes = keep.tile([P, PASSES * N], U32, name=f"w_codes{d}", align_bytes=64)
-            scale = keep.tile([P, PASSES * N], U8, name=f"w_scale{d}", align_bytes=64)
-            nc.vector.quantize_mx(out=codes[:].bitcast(FP8X4), scales=scale[:], in_=grouped[:].rearrange("p z m j -> p (z m j)"))
-            w_codes.append(codes)
-            w_scale.append(scale)
+        def quantize(raws, name, tag):
+            n = len(raws)
+            grouped = keep.tile([P, n, PASSES, N, PACK], BF16, name=f"grouped{name}", tag=tag, align_bytes=64)
+            for i, raw in enumerate(raws):
+                nc.scalar.copy(grouped[:, i], raw[:].rearrange("p z j m -> p z m j"))
+            codes = keep.tile([P, n * PASSES * N], U32, name=f"w_codes{name}", align_bytes=64)
+            scale = keep.tile([P, n * PASSES * N], U8, name=f"w_scale{name}", align_bytes=64)
+            nc.vector.quantize_mx(out=codes[:].bitcast(FP8X4), scales=scale[:], in_=grouped[:].rearrange("p i z m j -> p (i z m j)"))
+            return [(codes, scale, i * PASSES * N) for i in range(n)]
+
+        quantized = quantize(early, "early", "shared")
+        quantized = quantized + quantize([load_weight(2, "shared")], "late", "late")
+
+        x_second = []
+        for name, first, count in (("a", 0, 1), ("b", 1, 2)):
+            piece = keep.tile([P, count * V], U32, name=f"x_second{name}", align_bytes=64)
+            nc.vector.tensor_copy(piece[:], word_tables[1][:].bitcast(U32).indirect(picks[:, first * V // 16 : (first + count) * V // 16]))
+            x_second.extend(piece[:, i * V : (i + 1) * V] for i in range(count))
 
         for d in range(TAPS):
-            x_second = keep.tile([P, V], U32, name=f"x_second{d}", align_bytes=64)
-            nc.vector.tensor_copy(x_second[:], word_tables[1][:].bitcast(U32).indirect(picks[:, d * V // 16 : (d + 1) * V // 16]))
             cols = slice(d * V, (d + 1) * V)
+            codes, scale, at = quantized[d]
             acc = psum.tile([P, V], F32, name=f"acc{d}")
-            for z, codes in enumerate((x_first[:, cols], x_second[:])):
+            for z, moving in enumerate((x_first[:, cols], x_second[d])):
                 nc.tensor.matmul_mx(
                     out=acc[:],
-                    lhsT=w_codes[d][:, z * N : (z + 1) * N].bitcast(FP8X4),
-                    lhsT_scale=w_scale[d][:, z * N : (z + 1) * N],
-                    rhs=codes.bitcast(FP8X4),
+                    lhsT=codes[:, at + z * N : at + (z + 1) * N].bitcast(FP8X4),
+                    lhsT_scale=scale[:, at + z * N : at + (z + 1) * N],
+                    rhs=moving.bitcast(FP8X4),
                     rhs_scale=x_scale[4 * z : P, cols],
                     start=(z == 0),
                     stop=(z == PASSES - 1),
                 )
-            y = keep.tile([P, V], F32, name=f"y{d}", tag="shared0" if d == 1 else f"y{d}", align_bytes=64)
+            y = keep.tile([P, V], F32, name=f"y{d}", tag="shared" if d == 1 else f"y{d}", align_bytes=64)
             nc.scalar.copy(y[:], acc[:])
             nc.vector.tensor_copy(placed[d][:].indirect(maps[d][:]), y[:])
 

@@ -34,7 +34,7 @@ def tile_picked_spconv_none_p_kernel(tc, x_words, x_scales, w1, w2, w3, offs, to
         word_tables = [keep.tile([P, T], I32, name=f"word_table{z}", align_bytes=64) for z in range(PASSES)]
 
         nc.sync.dma_start(picks[:], offs)
-        nc.scalar.dma_start(scale_table[ROW0:P, :].bitcast(I32), x_scales.rearrange("z q c -> (z q) c").bitcast(I32))
+        nc.sync.dma_start(scale_table[ROW0:P, :].bitcast(I32), x_scales.rearrange("z q c -> (z q) c").bitcast(I32))
         nc.vector.memset(scale_table[0:ROW0, :].bitcast(I32), 0)
 
         def load_words(z):
@@ -45,14 +45,14 @@ def tile_picked_spconv_none_p_kernel(tc, x_words, x_scales, w1, w2, w3, offs, to
             nc.sync.dma_start(raw[:].rearrange("p z j m -> p z (j m)"), weights[d].rearrange("(z p j) m -> p z (j m)", z=PASSES, j=PACK))
             return raw
 
+        load_words(0)
         for tile, dram in zip(maps, (to1, to2, to3)):
             nc.sync.dma_start(tile[:], dram)
-        load_words(0)
         early = [load_weight(d, f"raw{d}") for d in range(2)]
         load_words(1)
 
         placed = [keep.tile([P, U], F32, name=f"placed{d}") for d in range(TAPS)]
-        x_scale = keep.tile([P, S], U8, name="x_scale", align_bytes=64)
+        x_scale = keep.tile([P, PASSES * S], U8, name="x_scale", align_bytes=64)
         nc.vector.memset(x_scale[:].bitcast(I32), 0)
         zero = keep.tile([P, 1], F32, name="zero")
         nc.vector.memset(zero[:], 0.0)
@@ -67,8 +67,7 @@ def tile_picked_spconv_none_p_kernel(tc, x_words, x_scales, w1, w2, w3, offs, to
         for z in range(PASSES):
             for q in range(4):
                 src = ROW0 + 16 * z + 4 * q
-                dst = 32 * q + 4 * z
-                nc.sync.dma_start(x_scale[dst : dst + 4, :].bitcast(I32), picked_rows[src : src + 4, :].bitcast(I32))
+                nc.sync.dma_start(x_scale[32 * q : 32 * q + 4, z * S : (z + 1) * S].bitcast(I32), picked_rows[src : src + 4, :].bitcast(I32))
         x_first = keep.tile([P, S], U32, name="x_first", align_bytes=64)
         nc.vector.tensor_copy(x_first[:], word_tables[0][:].bitcast(U32).indirect(picks[:]))
 
@@ -82,7 +81,7 @@ def tile_picked_spconv_none_p_kernel(tc, x_words, x_scales, w1, w2, w3, offs, to
             nc.vector.quantize_mx(out=codes[:].bitcast(FP8X4), scales=scale[:], in_=grouped[:].rearrange("p i z m j -> p (i z m j)"))
             return [(codes, scale, i * PASSES * N) for i in range(n)]
 
-        quantized = quantize(early, "early", "shared")
+        quantized = quantize(early[0:1], "first", "first") + quantize(early[1:2], "second", "shared")
         quantized = quantized + quantize([load_weight(2, "shared")], "late", "late")
 
         x_second = []
@@ -101,7 +100,7 @@ def tile_picked_spconv_none_p_kernel(tc, x_words, x_scales, w1, w2, w3, offs, to
                     lhsT=codes[:, at + z * N : at + (z + 1) * N].bitcast(FP8X4),
                     lhsT_scale=scale[:, at + z * N : at + (z + 1) * N],
                     rhs=moving.bitcast(FP8X4),
-                    rhs_scale=x_scale[4 * z : P, cols],
+                    rhs_scale=x_scale[:, z * S + d * V : z * S + (d + 1) * V],
                     start=(z == 0),
                     stop=(z == PASSES - 1),
                 )

@@ -53,7 +53,6 @@ def tile_picked_spconv_none_p_kernel(tc, x_words, x_scales, w1, w2, w3, offs, to
 
         placed = [keep.tile([P, U], F32, name=f"placed{d}") for d in range(TAPS)]
         x_scale = keep.tile([P, PASSES * S], U8, name="x_scale", align_bytes=64)
-        nc.vector.memset(x_scale[:].bitcast(I32), 0)
         zero = keep.tile([P, 1], F32, name="zero")
         nc.vector.memset(zero[:], 0.0)
         for d in range(TAPS):
@@ -130,5 +129,4 @@ def tile_picked_spconv_none_p_kernel(tc, x_words, x_scales, w1, w2, w3, offs, to
                 w = BANK // 2
                 total = keep.tile([P, w], F32, name=f"total{h}{c}")
                 nc.vector.tensor_tensor(total[:], pair[:, c * w : (c + 1) * w], placed[2][:, h * BANK + c * w : h * BANK + (c + 1) * w], mybir.AluOpType.add)
-                queue = nc.sync if c == 0 else nc.scalar
-                queue.dma_start(out[:, h * BANK + c * w : h * BANK + (c + 1) * w], total[:])
+                nc.sync.dma_start(out[:, h * BANK + c * w : h * BANK + (c + 1) * w], total[:])

@@ -30,7 +30,7 @@ def tile_picked_spconv_none_p_kernel(tc, x_words, x_scales, w1, w2, w3, offs, to
 
         picks = keep.tile([P, S // 16], U16, name="picks")
         maps = [keep.tile([P, V // 16], U16, name=f"map{d}") for d in range(TAPS)]
-        scale_table = keep.tile([P, T], U8, name="scale_table", align_bytes=64)
+        scale_table = keep.tile([P, T], U8, name="scale_table", tag="table", align_bytes=64)
         word_tables = [keep.tile([P, T], I32, name=f"word_table{z}", align_bytes=64) for z in range(PASSES)]
 
         nc.sync.dma_start(picks[:], offs)
@@ -48,11 +48,11 @@ def tile_picked_spconv_none_p_kernel(tc, x_words, x_scales, w1, w2, w3, offs, to
         load_words(0)
         for tile, dram in zip(maps, (to1, to2, to3)):
             nc.sync.dma_start(tile[:], dram)
-        early = [load_weight(d, f"raw{d}") for d in range(2)]
+        raw_first = load_weight(0, "raw0")
         load_words(1)
 
         placed = [keep.tile([P, U], F32, name=f"placed{d}") for d in range(TAPS)]
-        x_scale = keep.tile([P, PASSES * S], U8, name="x_scale", align_bytes=64)
+        x_scale = [keep.tile([P, S], U8, name=f"x_scale{z}", align_bytes=64) for z in range(PASSES)]
         zero = keep.tile([P, 1], F32, name="zero")
         nc.vector.memset(zero[:], 0.0)
         for d in range(TAPS):
@@ -63,10 +63,17 @@ def tile_picked_spconv_none_p_kernel(tc, x_words, x_scales, w1, w2, w3, offs, to
 
         picked_rows = keep.tile([P, S], U8, name="picked_rows", align_bytes=64)
         nc.vector.tensor_copy(picked_rows[:], scale_table[:].indirect(picks[:]))
-        for z in range(PASSES):
-            for q in range(4):
-                src = ROW0 + 16 * z + 4 * q
-                nc.sync.dma_start(x_scale[32 * q : 32 * q + 4, z * S : (z + 1) * S].bitcast(I32), picked_rows[src : src + 4, :].bitcast(I32))
+
+        def move_rows(z, q):
+            src = ROW0 + 16 * z + 4 * q
+            dst = 32 * q + 4 * z
+            nc.sync.dma_start(x_scale[z][dst : dst + 4, :].bitcast(I32), picked_rows[src : src + 4, :].bitcast(I32))
+
+        moves = [(z, q) for z in range(PASSES) for q in range(4)]
+        move_rows(*moves[0])
+        raw_second = load_weight(1, "table")
+        for z, q in moves[1:]:
+            move_rows(z, q)
         x_first = keep.tile([P, S], U32, name="x_first", align_bytes=64)
         nc.vector.tensor_copy(x_first[:], word_tables[0][:].bitcast(U32).indirect(picks[:]))
 
@@ -80,8 +87,8 @@ def tile_picked_spconv_none_p_kernel(tc, x_words, x_scales, w1, w2, w3, offs, to
             nc.vector.quantize_mx(out=codes[:].bitcast(FP8X4), scales=scale[:], in_=grouped[:].rearrange("p i z m j -> p (i z m j)"))
             return [(codes, scale, i * PASSES * N) for i in range(n)]
 
-        quantized = quantize(early[0:1], "first", "first") + quantize(early[1:2], "second", "shared")
-        quantized = quantized + quantize([load_weight(2, "shared")], "late", "late")
+        quantized = quantize([raw_first], "first", "shared")
+        raw_third = load_weight(2, "shared")
 
         x_second = []
         for name, first, count in (("a", 0, 1), ("b", 1, 2)):
@@ -89,21 +96,25 @@ def tile_picked_spconv_none_p_kernel(tc, x_words, x_scales, w1, w2, w3, offs, to
             nc.vector.tensor_copy(piece[:], word_tables[1][:].bitcast(U32).indirect(picks[:, first * V // 16 : (first + count) * V // 16]))
             x_second.extend(piece[:, i * V : (i + 1) * V] for i in range(count))
 
+        quantized = quantized + quantize([raw_second], "second", "second")
+
         for d in range(TAPS):
+            if d == 1:
+                quantized = quantized + quantize([raw_third], "third", "third")
             cols = slice(d * V, (d + 1) * V)
             codes, scale, at = quantized[d]
-            acc = psum.tile([P, V], F32, name=f"acc{d}")
+            acc = psum.tile([P, V], F32, name=f"acc{d}", tag=f"acc{d // 2}")
             for z, moving in enumerate((x_first[:, cols], x_second[d])):
                 nc.tensor.matmul_mx(
                     out=acc[:],
                     lhsT=codes[:, at + z * N : at + (z + 1) * N].bitcast(FP8X4),
                     lhsT_scale=scale[:, at + z * N : at + (z + 1) * N],
                     rhs=moving.bitcast(FP8X4),
-                    rhs_scale=x_scale[:, z * S + d * V : z * S + (d + 1) * V],
+                    rhs_scale=x_scale[z][4 * z :, cols],
                     start=(z == 0),
                     stop=(z == PASSES - 1),
                 )
-            y = keep.tile([P, V], F32, name=f"y{d}", tag="shared" if d == 1 else f"y{d}", align_bytes=64)
+            y = keep.tile([P, V], F32, name=f"y{d}", tag=("table", "shared", "y2")[d], align_bytes=64)
             nc.scalar.copy(y[:], acc[:])
             nc.vector.tensor_copy(placed[d][:].indirect(maps[d][:]), y[:])
 

@@ -33,8 +33,8 @@ def tile_picked_spconv_none_p_kernel(tc, x_words, x_scales, w1, w2, w3, offs, to
         scale_table = keep.tile([P, T], U8, name="scale_table", tag="table", align_bytes=64)
         word_tables = [keep.tile([P, T], I32, name=f"word_table{z}", align_bytes=64) for z in range(PASSES)]
 
-        nc.sync.dma_start(picks[:], offs)
         nc.sync.dma_start(scale_table[ROW0:P, :].bitcast(I32), x_scales.rearrange("z q c -> (z q) c").bitcast(I32))
+        nc.sync.dma_start(picks[:], offs)
         nc.vector.memset(scale_table[0:ROW0, :].bitcast(I32), 0)
 
         def load_words(z):
@@ -55,11 +55,12 @@ def tile_picked_spconv_none_p_kernel(tc, x_words, x_scales, w1, w2, w3, offs, to
         x_scale = [keep.tile([P, S], U8, name=f"x_scale{z}", align_bytes=64) for z in range(PASSES)]
         zero = keep.tile([P, 1], F32, name="zero")
         nc.vector.memset(zero[:], 0.0)
-        for d in range(TAPS):
-            nc.scalar.copy(placed[d][:], zero[:].to_broadcast([P, U]))
         ident = keep.tile([P, P], F32, name="ident")
         nc.vector.memset(ident[:], 0.0)
         make_identity(nc, ident[:], nomemset=True)
+        nc.vector.memset(placed[0][:], 0.0)
+        for d in range(1, TAPS):
+            nc.scalar.copy(placed[d][:], zero[:].to_broadcast([P, U]))
 
         picked_rows = keep.tile([P, S], U8, name="picked_rows", align_bytes=64)
         nc.vector.tensor_copy(picked_rows[:], scale_table[:].indirect(picks[:]))
@@ -119,20 +120,21 @@ def tile_picked_spconv_none_p_kernel(tc, x_words, x_scales, w1, w2, w3, offs, to
             nc.vector.tensor_copy(placed[d][:].indirect(maps[d][:]), y[:])
 
         blocks = BANK // P
-        for h in range(U // BANK):
-            turned = psum.tile([P, BANK], F32, name=f"turned{h}")
-            for d in range(2):
+        turned = [psum.tile([P, BANK], F32, name=f"turned{h}") for h in range(U // BANK)]
+        for d in range(2):
+            for h in range(U // BANK):
                 for b in range(blocks):
                     nc.tensor.matmul(
-                        turned[:, b * P : (b + 1) * P],
+                        turned[h][:, b * P : (b + 1) * P],
                         placed[d][:, h * BANK + b * P : h * BANK + (b + 1) * P],
                         ident[:],
                         start=(d == 0 and b == 0),
                         stop=(d == 1 and b == blocks - 1),
                         is_transpose=True,
                     )
+        for h in range(U // BANK):
             pair_t = keep.tile([P, BANK], F32, name=f"pair_t{h}")
-            nc.scalar.copy(pair_t[:], turned[:])
+            nc.scalar.copy(pair_t[:], turned[h][:])
             pair = psum.tile([P, BANK], F32, name=f"pair{h}")
             for b in range(blocks):
                 nc.tensor.transpose(pair[:, b * P : (b + 1) * P], pair_t[:, b * P : (b + 1) * P], ident[:])

@@ -119,27 +119,31 @@ def tile_picked_spconv_none_p_kernel(tc, x_words, x_scales, w1, w2, w3, offs, to
             nc.scalar.copy(y[:], acc[:])
             nc.vector.tensor_copy(placed[d][:].indirect(maps[d][:]), y[:])
 
-        blocks = BANK // P
-        turned = [psum.tile([P, BANK], F32, name=f"turned{h}") for h in range(U // BANK)]
+        piece_cols = BANK // 2
+        blocks = piece_cols // P
+        pieces = U // piece_cols
+        turned = [psum.tile([P, piece_cols], F32, name=f"turned{c}") for c in range(pieces)]
         for d in range(2):
-            for h in range(U // BANK):
+            for c in range(pieces):
                 for b in range(blocks):
                     nc.tensor.matmul(
-                        turned[h][:, b * P : (b + 1) * P],
-                        placed[d][:, h * BANK + b * P : h * BANK + (b + 1) * P],
+                        turned[c][:, b * P : (b + 1) * P],
+                        placed[d][:, c * piece_cols + b * P : c * piece_cols + (b + 1) * P],
                         ident[:],
                         start=(d == 0 and b == 0),
                         stop=(d == 1 and b == blocks - 1),
                         is_transpose=True,
                     )
-        for h in range(U // BANK):
-            pair_t = keep.tile([P, BANK], F32, name=f"pair_t{h}")
-            nc.scalar.copy(pair_t[:], turned[h][:])
-            pair = psum.tile([P, BANK], F32, name=f"pair{h}")
+        pair = [psum.tile([P, BANK], F32, name=f"pair{h}") for h in range(U // BANK)]
+        for c in range(pieces):
+            pair_t = keep.tile([P, piece_cols], F32, name=f"pair_t{c}")
+            nc.scalar.copy(pair_t[:], turned[c][:])
             for b in range(blocks):
-                nc.tensor.transpose(pair[:, b * P : (b + 1) * P], pair_t[:, b * P : (b + 1) * P], ident[:])
-            for c in range(2):
-                w = BANK // 2
-                total = keep.tile([P, w], F32, name=f"total{h}{c}")
-                nc.vector.tensor_tensor(total[:], pair[:, c * w : (c + 1) * w], placed[2][:, h * BANK + c * w : h * BANK + (c + 1) * w], mybir.AluOpType.add)
-                nc.sync.dma_start(out[:, h * BANK + c * w : h * BANK + (c + 1) * w], total[:])
+                at = (c % 2) * piece_cols + b * P
+                nc.tensor.transpose(pair[c // 2][:, at : at + P], pair_t[:, b * P : (b + 1) * P], ident[:])
+        for c in range(pieces):
+            cols = slice(c * piece_cols, (c + 1) * piece_cols)
+            at = (c % 2) * piece_cols
+            total = keep.tile([P, piece_cols], F32, name=f"total{c}")
+            nc.vector.tensor_tensor(total[:], pair[c // 2][:, at : at + piece_cols], placed[2][:, cols], mybir.AluOpType.add)
+            nc.sync.dma_start(out[:, cols], total[:])

@@ -1,7 +1,6 @@
 from contextlib import ExitStack
 
 import concourse.mybir as mybir
-from concourse.masks import make_identity
 
 K, T, S, V, N, U = 1024, 2048, 1536, 512, 128, 1024
 TAPS = 3
@@ -55,9 +54,6 @@ def tile_picked_spconv_none_p_kernel(tc, x_words, x_scales, w1, w2, w3, offs, to
         x_scale = [keep.tile([P, S], U8, name=f"x_scale{z}", align_bytes=64) for z in range(PASSES)]
         zero = keep.tile([P, 1], F32, name="zero")
         nc.vector.memset(zero[:], 0.0)
-        ident = keep.tile([P, P], F32, name="ident")
-        nc.vector.memset(ident[:], 0.0)
-        make_identity(nc, ident[:], nomemset=True)
         nc.vector.memset(placed[0][:], 0.0)
         for d in range(1, TAPS):
             nc.scalar.copy(placed[d][:], zero[:].to_broadcast([P, U]))
@@ -120,30 +116,10 @@ def tile_picked_spconv_none_p_kernel(tc, x_words, x_scales, w1, w2, w3, offs, to
             nc.vector.tensor_copy(placed[d][:].indirect(maps[d][:]), y[:])
 
         piece_cols = BANK // 2
-        blocks = piece_cols // P
-        pieces = U // piece_cols
-        turned = [psum.tile([P, piece_cols], F32, name=f"turned{c}") for c in range(pieces)]
-        for d in range(2):
-            for c in range(pieces):
-                for b in range(blocks):
-                    nc.tensor.matmul(
-                        turned[c][:, b * P : (b + 1) * P],
-                        placed[d][:, c * piece_cols + b * P : c * piece_cols + (b + 1) * P],
-                        ident[:],
-                        start=(d == 0 and b == 0),
-                        stop=(d == 1 and b == blocks - 1),
-                        is_transpose=True,
-                    )
-        pair = [psum.tile([P, BANK], F32, name=f"pair{h}") for h in range(U // BANK)]
-        for c in range(pieces):
-            pair_t = keep.tile([P, piece_cols], F32, name=f"pair_t{c}")
-            nc.scalar.copy(pair_t[:], turned[c][:])
-            for b in range(blocks):
-                at = (c % 2) * piece_cols + b * P
-                nc.tensor.transpose(pair[c // 2][:, at : at + P], pair_t[:, b * P : (b + 1) * P], ident[:])
-        for c in range(pieces):
+        for c in range(U // piece_cols):
             cols = slice(c * piece_cols, (c + 1) * piece_cols)
-            at = (c % 2) * piece_cols
+            pair = keep.tile([P, piece_cols], F32, name=f"pair{c}")
+            nc.gpsimd.tensor_tensor(pair[:], placed[0][:, cols], placed[1][:, cols], mybir.AluOpType.add)
             total = keep.tile([P, piece_cols], F32, name=f"total{c}")
-            nc.vector.tensor_tensor(total[:], pair[c // 2][:, at : at + piece_cols], placed[2][:, cols], mybir.AluOpType.add)
+            nc.vector.tensor_tensor(total[:], pair[:], placed[2][:, cols], mybir.AluOpType.add)
             nc.sync.dma_start(out[:, cols], total[:])

@@ -44,9 +44,9 @@ def tile_picked_spconv_none_p_kernel(tc, x_words, x_scales, w1, w2, w3, offs, to
             nc.sync.dma_start(raw[:].rearrange("p z j m -> p z (j m)"), weights[d].rearrange("(z p j) m -> p z (j m)", z=PASSES, j=PACK))
             return raw
 
-        load_words(0)
         for tile, dram in zip(maps, (to1, to2, to3)):
             nc.sync.dma_start(tile[:], dram)
+        load_words(0)
         raw_first = load_weight(0, "raw0")
         load_words(1)
 

@@ -7,8 +7,9 @@ TAPS = 3
 P = 128
 PACK = 4
 PASSES = K // (P * PACK)
-BANK = 512
+HALF = V // 2
 ROW0 = P - 16 * PASSES
+STORE_COLS = 256
 FLOPS = 2 * K * N * S
 
 F32 = mybir.dt.float32
@@ -18,6 +19,7 @@ U32 = mybir.dt.uint32
 U16 = mybir.dt.uint16
 U8 = mybir.dt.uint8
 FP8X4 = mybir.dt.float8_e4m3fn_x4
+ADD = mybir.AluOpType.add
 
 
 def tile_picked_spconv_none_p_kernel(tc, x_words, x_scales, w1, w2, w3, offs, to1, to2, to3, out):
@@ -27,38 +29,71 @@ def tile_picked_spconv_none_p_kernel(tc, x_words, x_scales, w1, w2, w3, offs, to
         keep = ctx.enter_context(tc.tile_pool(name="keep", bufs=1))
         psum = ctx.enter_context(tc.psum_pool(name="psum", bufs=1))
 
+        def sbuf(name, cols, dtype, tag=None):
+            return keep.tile([P, cols], dtype, name=name, tag=tag or name, align_bytes=64)
+
         picks = keep.tile([P, S // 16], U16, name="picks")
         maps = [keep.tile([P, V // 16], U16, name=f"map{d}") for d in range(TAPS)]
-        scale_table = keep.tile([P, T], U8, name="scale_table", tag="table", align_bytes=64)
-        word_tables = [keep.tile([P, T], I32, name=f"word_table{z}", align_bytes=64) for z in range(PASSES)]
-
-        nc.sync.dma_start(scale_table[ROW0:P, :].bitcast(I32), x_scales.rearrange("z q c -> (z q) c").bitcast(I32))
-        nc.sync.dma_start(picks[:], offs)
-        nc.vector.memset(scale_table[0:ROW0, :].bitcast(I32), 0)
+        scale_table = sbuf("scale_table", T, U8, "after_scales")
+        word_tables = [sbuf(f"word_table{z}", T, I32) for z in range(PASSES)]
+        placed = [sbuf(f"placed{d}", U, F32) for d in range(TAPS)]
+        x_scale = [sbuf(f"x_scale{z}", S, U8) for z in range(PASSES)]
 
         def load_words(z):
             nc.sync.dma_start(word_tables[z][:], x_words[z].rearrange("p c r -> p (c r)").bitcast(I32))
 
         def load_weight(d, tag):
-            raw = keep.tile([P, PASSES, PACK, N], F32, name=f"raw{d}", tag=tag, align_bytes=64)
-            nc.sync.dma_start(raw[:].rearrange("p z j m -> p z (j m)"), weights[d].rearrange("(z p j) m -> p z (j m)", z=PASSES, j=PACK))
+            raw = sbuf(f"raw{d}", PASSES * PACK * N, F32, tag)
+            nc.sync.dma_start(raw[:].rearrange("p (z r) -> p z r", z=PASSES), weights[d].rearrange("(z p j) m -> p z (j m)", z=PASSES, j=PACK))
             return raw
 
+        def quantize(d, raw, codes_tag, grouped_tag=None, scale_tag=None):
+            grouped = sbuf(f"grouped{d}", PASSES * N * PACK, BF16, grouped_tag)
+            nc.scalar.copy(grouped[:].rearrange("p (z m j) -> p z m j", z=PASSES, j=PACK), raw[:].rearrange("p (z j m) -> p z m j", z=PASSES, j=PACK))
+            codes = sbuf(f"w_codes{d}", PASSES * N, U32, codes_tag)
+            scale = sbuf(f"w_scale{d}", PASSES * N, U8, scale_tag)
+            nc.vector.quantize_mx(out=codes[:].bitcast(FP8X4), scales=scale[:], in_=grouped[:])
+            return codes, scale
+
+        def gather_words(z, first, count, tag=None):
+            piece = sbuf(f"x{z}_{first}", count, U32, tag)
+            nc.vector.tensor_copy(piece[:], word_tables[z][:].bitcast(U32).indirect(picks[:, first // 16 : (first + count) // 16]))
+            return piece
+
+        def product(acc, quantized, first, moving):
+            codes, scale = quantized
+            count = acc.shape[1]
+            for z in range(PASSES):
+                nc.tensor.matmul_mx(
+                    out=acc,
+                    lhsT=codes[:, z * N : (z + 1) * N].bitcast(FP8X4),
+                    lhsT_scale=scale[:, z * N : (z + 1) * N],
+                    rhs=moving[z].bitcast(FP8X4),
+                    rhs_scale=x_scale[z][4 * z :, first : first + count],
+                    start=(z == 0),
+                    stop=(z == PASSES - 1),
+                )
+
+        def scatter(d, first, values):
+            count = values.shape[1]
+            nc.vector.tensor_copy(placed[d][:].indirect(maps[d][:, first // 16 : (first + count) // 16]), values)
+
+        nc.sync.dma_start(scale_table[ROW0:P, :].bitcast(I32), x_scales.rearrange("z q c -> (z q) c").bitcast(I32))
+        nc.sync.dma_start(picks[:], offs)
+        nc.vector.memset(scale_table[0:ROW0, :].bitcast(I32), 0)
         for tile, dram in zip(maps, (to1, to2, to3)):
             nc.sync.dma_start(tile[:], dram)
         load_words(0)
-        raw_first = load_weight(0, "raw0")
+        raw0 = load_weight(0, "raw0")
         load_words(1)
 
-        placed = [keep.tile([P, U], F32, name=f"placed{d}") for d in range(TAPS)]
-        x_scale = [keep.tile([P, S], U8, name=f"x_scale{z}", align_bytes=64) for z in range(PASSES)]
-        zero = keep.tile([P, 1], F32, name="zero")
+        zero = sbuf("zero", 1, F32)
         nc.vector.memset(zero[:], 0.0)
         nc.vector.memset(placed[0][:], 0.0)
         for d in range(1, TAPS):
             nc.scalar.copy(placed[d][:], zero[:].to_broadcast([P, U]))
 
-        picked_rows = keep.tile([P, S], U8, name="picked_rows", align_bytes=64)
+        picked_rows = sbuf("picked_rows", S, U8)
         nc.vector.tensor_copy(picked_rows[:], scale_table[:].indirect(picks[:]))
 
         def move_rows(z, q):
@@ -68,58 +103,51 @@ def tile_picked_spconv_none_p_kernel(tc, x_words, x_scales, w1, w2, w3, offs, to
 
         moves = [(z, q) for z in range(PASSES) for q in range(4)]
         move_rows(*moves[0])
-        raw_second = load_weight(1, "table")
+        raw1 = load_weight(1, "after_scales")
         for z, q in moves[1:]:
             move_rows(z, q)
-        x_first = keep.tile([P, S], U32, name="x_first", align_bytes=64)
-        nc.vector.tensor_copy(x_first[:], word_tables[0][:].bitcast(U32).indirect(picks[:]))
 
-        def quantize(raws, name, tag):
-            n = len(raws)
-            grouped = keep.tile([P, n, PASSES, N, PACK], BF16, name=f"grouped{name}", tag=tag, align_bytes=64)
-            for i, raw in enumerate(raws):
-                nc.scalar.copy(grouped[:, i], raw[:].rearrange("p z j m -> p z m j"))
-            codes = keep.tile([P, n * PASSES * N], U32, name=f"w_codes{name}", align_bytes=64)
-            scale = keep.tile([P, n * PASSES * N], U8, name=f"w_scale{name}", align_bytes=64)
-            nc.vector.quantize_mx(out=codes[:].bitcast(FP8X4), scales=scale[:], in_=grouped[:].rearrange("p i z m j -> p (i z m j)"))
-            return [(codes, scale, i * PASSES * N) for i in range(n)]
+        x0_early = gather_words(0, 0, 2 * V)
+        q0 = quantize(0, raw0, "codes0", "after_first_quantise")
+        raw2 = load_weight(2, "after_first_quantise")
+        x1_tap0 = gather_words(1, 0, V, "after_tap0")
+        x1_rest = gather_words(1, V, 2 * V)
+        q1 = quantize(1, raw1, "codes1", None, "after_tap1")
 
-        quantized = quantize([raw_first], "first", "shared")
-        raw_third = load_weight(2, "shared")
+        def leave(acc, name, tag=None):
+            y = sbuf(name, acc.shape[1], F32, tag)
+            nc.scalar.copy(y[:], acc)
+            return y
 
-        x_second = []
-        for name, first, count in (("a", 0, 1), ("b", 1, 2)):
-            piece = keep.tile([P, count * V], U32, name=f"x_second{name}", align_bytes=64)
-            nc.vector.tensor_copy(piece[:], word_tables[1][:].bitcast(U32).indirect(picks[:, first * V // 16 : (first + count) * V // 16]))
-            x_second.extend(piece[:, i * V : (i + 1) * V] for i in range(count))
+        y0 = []
+        for h in range(2):
+            cols = slice(h * HALF, (h + 1) * HALF)
+            acc = psum.tile([P, HALF], F32, name=f"acc0_{h}", tag="chain")
+            product(acc[:], q0, h * HALF, (x0_early[:, cols], x1_tap0[:, cols]))
+            y0.append(leave(acc[:], f"y0_{h}", "after_scales" if h == 0 else None))
+        acc1 = psum.tile([P, V], F32, name="acc1", tag="chain")
+        product(acc1[:], q1, V, (x0_early[:, V : 2 * V], x1_rest[:, 0:V]))
 
-        quantized = quantized + quantize([raw_second], "second", "second")
+        x0_late = []
+        for h in range(2):
+            scatter(0, h * HALF, y0[h][:])
+            x0_late.append(gather_words(0, 2 * V + h * HALF, HALF, f"codes{h}"))
 
-        for d in range(TAPS):
-            if d == 1:
-                quantized = quantized + quantize([raw_third], "third", "third")
-            cols = slice(d * V, (d + 1) * V)
-            codes, scale, at = quantized[d]
-            acc = psum.tile([P, V], F32, name=f"acc{d}", tag=f"acc{d // 2}")
-            for z, moving in enumerate((x_first[:, cols], x_second[d])):
-                nc.tensor.matmul_mx(
-                    out=acc[:],
-                    lhsT=codes[:, at + z * N : at + (z + 1) * N].bitcast(FP8X4),
-                    lhsT_scale=scale[:, at + z * N : at + (z + 1) * N],
-                    rhs=moving.bitcast(FP8X4),
-                    rhs_scale=x_scale[z][4 * z :, cols],
-                    start=(z == 0),
-                    stop=(z == PASSES - 1),
-                )
-            y = keep.tile([P, V], F32, name=f"y{d}", tag=("table", "shared", "y2")[d], align_bytes=64)
-            nc.scalar.copy(y[:], acc[:])
-            nc.vector.tensor_copy(placed[d][:].indirect(maps[d][:]), y[:])
+        q2 = quantize(2, raw2, "codes2", "after_tap0", "after_tap1")
+        y1 = leave(acc1[:], "y1", "after_first_quantise")
+        scatter(1, 0, y1[:])
 
-        piece_cols = BANK // 2
-        for c in range(U // piece_cols):
-            cols = slice(c * piece_cols, (c + 1) * piece_cols)
-            pair = keep.tile([P, piece_cols], F32, name=f"pair{c}")
-            nc.gpsimd.tensor_tensor(pair[:], placed[0][:, cols], placed[1][:, cols], mybir.AluOpType.add)
-            total = keep.tile([P, piece_cols], F32, name=f"total{c}")
-            nc.vector.tensor_tensor(total[:], pair[:], placed[2][:, cols], mybir.AluOpType.add)
+        acc2 = psum.tile([P, V], F32, name="acc2")
+        for h in range(2):
+            cols = slice(h * HALF, (h + 1) * HALF)
+            product(acc2[:, cols], q2, 2 * V + h * HALF, (x0_late[h][:], x1_rest[:, V + h * HALF : V + (h + 1) * HALF]))
+        y2 = leave(acc2[:], "y2")
+        scatter(2, 0, y2[:])
+
+        for c in range(U // STORE_COLS):
+            cols = slice(c * STORE_COLS, (c + 1) * STORE_COLS)
+            pair = sbuf(f"pair{c}", STORE_COLS, F32)
+            nc.gpsimd.tensor_tensor(pair[:], placed[0][:, cols], placed[1][:, cols], ADD)
+            total = sbuf(f"total{c}", STORE_COLS, F32)
+            nc.vector.tensor_tensor(total[:], pair[:], placed[2][:, cols], ADD)
             nc.sync.dma_start(out[:, cols], total[:])

@@ -8,6 +8,7 @@ P = 128
 PACK = 4
 PASSES = K // (P * PACK)
 HALF = V // 2
+CHUNK = 128
 ROW0 = P - 16 * PASSES
 STORE_COLS = 256
 FLOPS = 2 * K * N * S
@@ -47,31 +48,35 @@ def tile_picked_spconv_none_p_kernel(tc, x_words, x_scales, w1, w2, w3, offs, to
             nc.sync.dma_start(raw[:].rearrange("p (z r) -> p z r", z=PASSES), weights[d].rearrange("(z p j) m -> p z (j m)", z=PASSES, j=PACK))
             return raw
 
-        def quantize(d, raw, codes_tag, grouped_tag=None, scale_tag=None):
+        def quantize(d, raw, pieces, grouped_tag, codes_tag=None):
             grouped = sbuf(f"grouped{d}", PASSES * N * PACK, BF16, grouped_tag)
-            nc.scalar.copy(grouped[:].rearrange("p (z m j) -> p z m j", z=PASSES, j=PACK), raw[:].rearrange("p (z j m) -> p z m j", z=PASSES, j=PACK))
+            src = raw[:].rearrange("p (z j m) -> p z m j", z=PASSES, j=PACK)
+            dst = grouped[:].rearrange("p (z m j) -> p z m j", z=PASSES, j=PACK)
+            step = PASSES // pieces
+            for z in range(0, PASSES, step):
+                nc.scalar.copy(dst[:, z : z + step], src[:, z : z + step])
             codes = sbuf(f"w_codes{d}", PASSES * N, U32, codes_tag)
-            scale = sbuf(f"w_scale{d}", PASSES * N, U8, scale_tag)
+            scale = sbuf(f"w_scale{d}", PASSES * N, U8)
             nc.vector.quantize_mx(out=codes[:].bitcast(FP8X4), scales=scale[:], in_=grouped[:])
             return codes, scale
 
-        def gather_words(z, first, count, tag=None):
-            piece = sbuf(f"x{z}_{first}", count, U32, tag)
-            nc.vector.tensor_copy(piece[:], word_tables[z][:].bitcast(U32).indirect(picks[:, first // 16 : (first + count) // 16]))
+        def gather_words(z, first, piece):
+            count = piece.shape[1]
+            nc.vector.tensor_copy(piece, word_tables[z][:].bitcast(U32).indirect(picks[:, first // 16 : (first + count) // 16]))
             return piece
 
-        def product(acc, quantized, first, moving):
+        def product(acc, quantized, first, moving, passes):
             codes, scale = quantized
             count = acc.shape[1]
-            for z in range(PASSES):
+            for z in passes:
                 nc.tensor.matmul_mx(
                     out=acc,
                     lhsT=codes[:, z * N : (z + 1) * N].bitcast(FP8X4),
                     lhsT_scale=scale[:, z * N : (z + 1) * N],
                     rhs=moving[z].bitcast(FP8X4),
                     rhs_scale=x_scale[z][4 * z :, first : first + count],
-                    start=(z == 0),
-                    stop=(z == PASSES - 1),
+                    start=(z == passes[0]),
+                    stop=(z == passes[-1]),
                 )
 
         def scatter(d, first, values):
@@ -81,9 +86,9 @@ def tile_picked_spconv_none_p_kernel(tc, x_words, x_scales, w1, w2, w3, offs, to
         nc.sync.dma_start(scale_table[ROW0:P, :].bitcast(I32), x_scales.rearrange("z q c -> (z q) c").bitcast(I32))
         nc.sync.dma_start(picks[:], offs)
         nc.vector.memset(scale_table[0:ROW0, :].bitcast(I32), 0)
+        load_words(0)
         for tile, dram in zip(maps, (to1, to2, to3)):
             nc.sync.dma_start(tile[:], dram)
-        load_words(0)
         raw0 = load_weight(0, "raw0")
         load_words(1)
 
@@ -102,47 +107,58 @@ def tile_picked_spconv_none_p_kernel(tc, x_words, x_scales, w1, w2, w3, offs, to
             nc.sync.dma_start(x_scale[z][dst : dst + 4, :].bitcast(I32), picked_rows[src : src + 4, :].bitcast(I32))
 
         moves = [(z, q) for z in range(PASSES) for q in range(4)]
-        move_rows(*moves[0])
+        for z, q in moves[:6]:
+            move_rows(z, q)
         raw1 = load_weight(1, "after_scales")
-        for z, q in moves[1:]:
+        for z, q in moves[6:]:
             move_rows(z, q)
 
-        x0_early = gather_words(0, 0, 2 * V)
-        q0 = quantize(0, raw0, "codes0", "after_first_quantise")
+        words_a = sbuf("words_a", 2 * V, U32)
+        words_first = sbuf("words_first", HALF, U32, "after_two_chunks")
+        words_b = sbuf("words_b", CHUNK + V, U32)
+        gather_words(0, 0, words_a[:])
+        quantized = [quantize(0, raw0, 1, "after_first_quantise", "after_tap0")]
         raw2 = load_weight(2, "after_first_quantise")
-        x1_tap0 = gather_words(1, 0, V, "after_tap0")
-        x1_rest = gather_words(1, V, 2 * V)
-        q1 = quantize(1, raw1, "codes1", None, "after_tap1")
+        gather_words(1, 0, words_first[:])
+        gather_words(1, HALF, words_b[:, CHUNK:])
 
-        def leave(acc, name, tag=None):
-            y = sbuf(name, acc.shape[1], F32, tag)
-            nc.scalar.copy(y[:], acc)
-            return y
+        def multiply(d, first, moving, y, bank):
+            acc = psum.tile([P, y.shape[1]], F32, name=f"acc{first}", tag=bank)
+            product(acc[:], quantized[d], first, moving, (0, 1))
+            nc.scalar.copy(y, acc[:])
 
-        y0 = []
-        for h in range(2):
-            cols = slice(h * HALF, (h + 1) * HALF)
-            acc = psum.tile([P, HALF], F32, name=f"acc0_{h}", tag="chain")
-            product(acc[:], q0, h * HALF, (x0_early[:, cols], x1_tap0[:, cols]))
-            y0.append(leave(acc[:], f"y0_{h}", "after_scales" if h == 0 else None))
-        acc1 = psum.tile([P, V], F32, name="acc1", tag="chain")
-        product(acc1[:], q1, V, (x0_early[:, V : 2 * V], x1_rest[:, 0:V]))
+        late = [
+            (1, 768, words_a[:, 0:256]),
+            (0, 1024, words_b[:, 0:256]),
+            (1, 1024, words_a[:, 256:512]),
+            (0, 1280, words_b[:, 256:512]),
+            (1, 1280, words_a[:, 512:768]),
+        ]
+        y_early = sbuf("y_early", 5 * CHUNK, F32)
 
-        x0_late = []
-        for h in range(2):
-            scatter(0, h * HALF, y0[h][:])
-            x0_late.append(gather_words(0, 2 * V + h * HALF, HALF, f"codes{h}"))
+        def chunk_product(k, y):
+            cols = slice(k * CHUNK, (k + 1) * CHUNK)
+            second = words_first[:, cols] if k < 2 else words_b[:, (k - 1) * CHUNK : k * CHUNK]
+            multiply(k * CHUNK // V, k * CHUNK, (words_a[:, cols], second), y, "chain")
 
-        q2 = quantize(2, raw2, "codes2", "after_tap0", "after_tap1")
-        y1 = leave(acc1[:], "y1", "after_first_quantise")
-        scatter(1, 0, y1[:])
-
-        acc2 = psum.tile([P, V], F32, name="acc2")
-        for h in range(2):
-            cols = slice(h * HALF, (h + 1) * HALF)
-            product(acc2[:, cols], q2, 2 * V + h * HALF, (x0_late[h][:], x1_rest[:, V + h * HALF : V + (h + 1) * HALF]))
-        y2 = leave(acc2[:], "y2")
-        scatter(2, 0, y2[:])
+        chunk_product(0, y_early[:, 0:CHUNK])
+        for k, (z, entry, piece) in enumerate(late):
+            if k == 3:
+                quantized.append(quantize(1, raw1, 2, "after_two_chunks"))
+            if k + 1 < len(late):
+                chunk_product(k + 1, y_early[:, (k + 1) * CHUNK : (k + 2) * CHUNK])
+            else:
+                quantized.append(quantize(2, raw2, 2, "after_tap0"))
+                y_rest = sbuf("y_rest", V - CHUNK, F32, "after_first_quantise")
+                chunk_product(k + 1, y_rest[:, 0:CHUNK])
+                multiply(1, 768, (words_a[:, 768:1024], words_a[:, 0:256]), y_rest[:, CHUNK:], "rest")
+            d, at = divmod(k * CHUNK, V)
+            scatter(d, at, y_early[:, k * CHUNK : (k + 1) * CHUNK])
+            gather_words(z, entry, piece)
+        scatter(1, CHUNK, y_rest[:])
+        y_last = sbuf("y_last", V, F32)
+        multiply(2, 2 * V, (words_b[:, 0:V], words_a[:, HALF : HALF + V]), y_last[:], "last")
+        scatter(2, 0, y_last[:])
 
         for c in range(U // STORE_COLS):
             cols = slice(c * STORE_COLS, (c + 1) * STORE_COLS)

@@ -48,13 +48,14 @@ def tile_picked_spconv_none_p_kernel(tc, x_words, x_scales, w1, w2, w3, offs, to
             nc.sync.dma_start(raw[:].rearrange("p (z r) -> p z r", z=PASSES), weights[d].rearrange("(z p j) m -> p z (j m)", z=PASSES, j=PACK))
             return raw
 
-        def quantize(d, raw, pieces, grouped_tag, codes_tag=None):
+        def quantize(d, raw, grouped_tag, codes_tag):
             grouped = sbuf(f"grouped{d}", PASSES * N * PACK, BF16, grouped_tag)
             src = raw[:].rearrange("p (z j m) -> p z m j", z=PASSES, j=PACK)
             dst = grouped[:].rearrange("p (z m j) -> p z m j", z=PASSES, j=PACK)
-            step = PASSES // pieces
-            for z in range(0, PASSES, step):
-                nc.scalar.copy(dst[:, z : z + step], src[:, z : z + step])
+            if d == 0:
+                nc.scalar.copy(dst, src)
+            else:
+                nc.gpsimd.tensor_scalar(dst, src, 1.0, 0.0, mybir.AluOpType.mult, ADD)
             codes = sbuf(f"w_codes{d}", PASSES * N, U32, codes_tag)
             scale = sbuf(f"w_scale{d}", PASSES * N, U8)
             nc.vector.quantize_mx(out=codes[:].bitcast(FP8X4), scales=scale[:], in_=grouped[:])
@@ -101,63 +102,65 @@ def tile_picked_spconv_none_p_kernel(tc, x_words, x_scales, w1, w2, w3, offs, to
         picked_rows = sbuf("picked_rows", S, U8)
         nc.vector.tensor_copy(picked_rows[:], scale_table[:].indirect(picks[:]))
 
-        def move_rows(z, q):
-            src = ROW0 + 16 * z + 4 * q
-            dst = 32 * q + 4 * z
-            nc.sync.dma_start(x_scale[z][dst : dst + 4, :].bitcast(I32), picked_rows[src : src + 4, :].bitcast(I32))
+        def move_rows(queue, z, i):
+            src = ROW0 + 16 * z + i
+            queue.dma_start(x_scale[z][4 * z + i : P : 32, :].bitcast(I32), picked_rows[src : src + 13 : 4, :].bitcast(I32))
 
-        moves = [(z, q) for z in range(PASSES) for q in range(4)]
-        for z, q in moves[:6]:
-            move_rows(z, q)
+        moves = [(z, i) for i in range(4) for z in range(PASSES)]
+        for z, i in moves[:-1]:
+            move_rows(nc.sync, z, i)
+        move_rows(nc.gpsimd, *moves[-1])
         raw1 = load_weight(1, "after_scales")
-        for z, q in moves[6:]:
-            move_rows(z, q)
 
         words_a = sbuf("words_a", 2 * V, U32)
-        words_first = sbuf("words_first", HALF, U32, "after_two_chunks")
-        words_b = sbuf("words_b", CHUNK + V, U32)
+        words_first = sbuf("words_first", HALF, U32)
+        words_b = sbuf("words_b", V + HALF, U32)
         gather_words(0, 0, words_a[:])
-        quantized = [quantize(0, raw0, 1, "after_first_quantise", "after_tap0")]
+        quantized = [quantize(0, raw0, "after_first_quantise", "codes_early")]
         raw2 = load_weight(2, "after_first_quantise")
         gather_words(1, 0, words_first[:])
-        gather_words(1, HALF, words_b[:, CHUNK:])
+        gather_words(1, HALF, words_b[:])
 
-        def multiply(d, first, moving, y, bank):
+        def multiply(first, moving, y, bank):
             acc = psum.tile([P, y.shape[1]], F32, name=f"acc{first}", tag=bank)
-            product(acc[:], quantized[d], first, moving, (0, 1))
+            product(acc[:], quantized[first // V], first, moving, (0, 1))
             nc.scalar.copy(y, acc[:])
 
-        late = [
-            (1, 768, words_a[:, 0:256]),
-            (0, 1024, words_b[:, 0:256]),
-            (1, 1024, words_a[:, 256:512]),
-            (0, 1280, words_b[:, 256:512]),
-            (1, 1280, words_a[:, 512:768]),
-        ]
-        y_early = sbuf("y_early", 5 * CHUNK, F32)
+        def early_product(first, y, bank):
+            end = first + y.shape[1]
+            second = words_first[:, first:end] if first < HALF else words_b[:, first - HALF : end - HALF]
+            multiply(first, (words_a[:, first:end], second), y, bank)
 
-        def chunk_product(k, y):
-            cols = slice(k * CHUNK, (k + 1) * CHUNK)
-            second = words_first[:, cols] if k < 2 else words_b[:, (k - 1) * CHUNK : k * CHUNK]
-            multiply(k * CHUNK // V, k * CHUNK, (words_a[:, cols], second), y, "chain")
-
-        chunk_product(0, y_early[:, 0:CHUNK])
-        for k, (z, entry, piece) in enumerate(late):
-            if k == 3:
-                quantized.append(quantize(1, raw1, 2, "after_two_chunks"))
-            if k + 1 < len(late):
-                chunk_product(k + 1, y_early[:, (k + 1) * CHUNK : (k + 2) * CHUNK])
-            else:
-                quantized.append(quantize(2, raw2, 2, "after_tap0"))
-                y_rest = sbuf("y_rest", V - CHUNK, F32, "after_first_quantise")
-                chunk_product(k + 1, y_rest[:, 0:CHUNK])
-                multiply(1, 768, (words_a[:, 768:1024], words_a[:, 0:256]), y_rest[:, CHUNK:], "rest")
-            d, at = divmod(k * CHUNK, V)
-            scatter(d, at, y_early[:, k * CHUNK : (k + 1) * CHUNK])
+        def scatter_then_gather(first, y, z, entry, piece):
+            scatter(first // V, first % V, y)
             gather_words(z, entry, piece)
+
+        y_a = sbuf("y_a", HALF, F32)
+        early_product(0, y_a[:, 0:CHUNK], "chain")
+        early_product(CHUNK, y_a[:, CHUNK:HALF], "chain")
+        scatter_then_gather(0, y_a[:, 0:CHUNK], 0, 2 * V, words_a[:, 0:HALF])
+
+        quantized.append(None)
+        acc_b = psum.tile([P, HALF], F32, name="acc_b", tag="chain")
+        product(acc_b[:], quantized[0], HALF, (words_a[:, HALF:V], words_b[:, 0:HALF]), (0, 1))
+        scatter_then_gather(CHUNK, y_a[:, CHUNK:HALF], 0, 2 * V + HALF, words_a[:, HALF:V])
+
+        quantized[1] = quantize(1, raw1, "grouped_late", "codes_early")
+        y_b = sbuf("y_b", HALF, F32, "after_scales")
+        nc.scalar.copy(y_b[:], acc_b[:])
+        y_c = sbuf("y_c", CHUNK, F32)
+        early_product(V, y_c[:], "chain")
+        scatter_then_gather(HALF, y_b[:], 1, 2 * V, words_b[:, CHUNK : CHUNK + HALF])
+
+        quantized.append(quantize(2, raw2, "grouped_late", None))
+        y_rest = sbuf("y_rest", V - CHUNK, F32, "after_first_quantise")
+        early_product(V + CHUNK, y_rest[:, 0:CHUNK], "chain")
+        early_product(V + HALF, y_rest[:, CHUNK:], "rest")
+        scatter_then_gather(V, y_c[:], 1, 2 * V + HALF, words_b[:, CHUNK + HALF : CHUNK + V])
+
         scatter(1, CHUNK, y_rest[:])
         y_last = sbuf("y_last", V, F32)
-        multiply(2, 2 * V, (words_b[:, 0:V], words_a[:, HALF : HALF + V]), y_last[:], "last")
+        multiply(2 * V, (words_a[:, 0:V], words_b[:, CHUNK : CHUNK + V]), y_last[:], "last")
         scatter(2, 0, y_last[:])
 
         for c in range(U // STORE_COLS):

@@ -48,16 +48,16 @@ def tile_picked_spconv_none_p_kernel(tc, x_words, x_scales, w1, w2, w3, offs, to
             nc.sync.dma_start(raw[:].rearrange("p (z r) -> p z r", z=PASSES), weights[d].rearrange("(z p j) m -> p z (j m)", z=PASSES, j=PACK))
             return raw
 
-        def quantize(d, raw, grouped_tag, codes_tag):
+        def quantize(d, raw, grouped_tag, scale_tag=None):
             grouped = sbuf(f"grouped{d}", PASSES * N * PACK, BF16, grouped_tag)
             src = raw[:].rearrange("p (z j m) -> p z m j", z=PASSES, j=PACK)
             dst = grouped[:].rearrange("p (z m j) -> p z m j", z=PASSES, j=PACK)
-            if d == 0:
-                nc.scalar.copy(dst, src)
-            else:
+            if d == 1:
                 nc.gpsimd.tensor_scalar(dst, src, 1.0, 0.0, mybir.AluOpType.mult, ADD)
-            codes = sbuf(f"w_codes{d}", PASSES * N, U32, codes_tag)
-            scale = sbuf(f"w_scale{d}", PASSES * N, U8)
+            else:
+                nc.scalar.copy(dst, src)
+            codes = sbuf(f"w_codes{d}", PASSES * N, U32, "codes")
+            scale = sbuf(f"w_scale{d}", PASSES * N, U8, scale_tag)
             nc.vector.quantize_mx(out=codes[:].bitcast(FP8X4), scales=scale[:], in_=grouped[:])
             return codes, scale
 
@@ -113,13 +113,12 @@ def tile_picked_spconv_none_p_kernel(tc, x_words, x_scales, w1, w2, w3, offs, to
         raw1 = load_weight(1, "after_scales")
 
         words_a = sbuf("words_a", 2 * V, U32)
-        words_first = sbuf("words_first", HALF, U32)
-        words_b = sbuf("words_b", V + HALF, U32)
+        words_b = sbuf("words_b", 2 * V, U32)
         gather_words(0, 0, words_a[:])
-        quantized = [quantize(0, raw0, "after_first_quantise", "codes_early")]
+        quantized = [quantize(0, raw0, "after_first_quantise", "after_tap0")]
         raw2 = load_weight(2, "after_first_quantise")
-        gather_words(1, 0, words_first[:])
-        gather_words(1, HALF, words_b[:])
+        gather_words(1, 0, words_b[:, 0:HALF])
+        gather_words(1, HALF, words_b[:, HALF:])
 
         def multiply(first, moving, y, bank):
             acc = psum.tile([P, y.shape[1]], F32, name=f"acc{first}", tag=bank)
@@ -128,40 +127,27 @@ def tile_picked_spconv_none_p_kernel(tc, x_words, x_scales, w1, w2, w3, offs, to
 
         def early_product(first, y, bank):
             end = first + y.shape[1]
-            second = words_first[:, first:end] if first < HALF else words_b[:, first - HALF : end - HALF]
-            multiply(first, (words_a[:, first:end], second), y, bank)
+            multiply(first, (words_a[:, first:end], words_b[:, first:end]), y, bank)
 
-        def scatter_then_gather(first, y, z, entry, piece):
-            scatter(first // V, first % V, y)
-            gather_words(z, entry, piece)
+        ys = [sbuf(f"y{d}", V, F32) for d in range(TAPS)]
+        late = [words_a[:, 0:V], words_b[:, CHUNK : CHUNK + V]]
+        early_product(0, ys[0][:, 0:CHUNK], "chain")
+        for k in range(4):
+            at = (k + 1) * CHUNK
+            if k == 3:
+                quantized.append(quantize(1, raw1, None))
+            early_product(at, ys[at // V][:, at % V : at % V + CHUNK], "chain")
+            scatter(0, k * CHUNK, ys[0][:, k * CHUNK : at])
+            half, z = divmod(k, PASSES)
+            gather_words(z, 2 * V + half * HALF, late[z][:, half * HALF : (half + 1) * HALF])
 
-        y_a = sbuf("y_a", HALF, F32)
-        early_product(0, y_a[:, 0:CHUNK], "chain")
-        early_product(CHUNK, y_a[:, CHUNK:HALF], "chain")
-        scatter_then_gather(0, y_a[:, 0:CHUNK], 0, 2 * V, words_a[:, 0:HALF])
-
-        quantized.append(None)
-        acc_b = psum.tile([P, HALF], F32, name="acc_b", tag="chain")
-        product(acc_b[:], quantized[0], HALF, (words_a[:, HALF:V], words_b[:, 0:HALF]), (0, 1))
-        scatter_then_gather(CHUNK, y_a[:, CHUNK:HALF], 0, 2 * V + HALF, words_a[:, HALF:V])
-
-        quantized[1] = quantize(1, raw1, "grouped_late", "codes_early")
-        y_b = sbuf("y_b", HALF, F32, "after_scales")
-        nc.scalar.copy(y_b[:], acc_b[:])
-        y_c = sbuf("y_c", CHUNK, F32)
-        early_product(V, y_c[:], "chain")
-        scatter_then_gather(HALF, y_b[:], 1, 2 * V, words_b[:, CHUNK : CHUNK + HALF])
-
-        quantized.append(quantize(2, raw2, "grouped_late", None))
-        y_rest = sbuf("y_rest", V - CHUNK, F32, "after_first_quantise")
-        early_product(V + CHUNK, y_rest[:, 0:CHUNK], "chain")
-        early_product(V + HALF, y_rest[:, CHUNK:], "rest")
-        scatter_then_gather(V, y_c[:], 1, 2 * V + HALF, words_b[:, CHUNK + HALF : CHUNK + V])
-
-        scatter(1, CHUNK, y_rest[:])
-        y_last = sbuf("y_last", V, F32)
-        multiply(2 * V, (words_a[:, 0:V], words_b[:, CHUNK : CHUNK + V]), y_last[:], "last")
-        scatter(2, 0, y_last[:])
+        early_product(V + HALF, ys[1][:, HALF:V], "rest")
+        early_product(V + CHUNK, ys[1][:, CHUNK:HALF], "chain")
+        scatter(1, 0, ys[1][:, 0:CHUNK])
+        quantized.append(quantize(2, raw2, "after_tap0"))
+        scatter(1, CHUNK, ys[1][:, CHUNK:V])
+        multiply(2 * V, late, ys[2][:], "last")
+        scatter(2, 0, ys[2][:])
 
         for c in range(U // STORE_COLS):
             cols = slice(c * STORE_COLS, (c + 1) * STORE_COLS)

@@ -40,24 +40,24 @@ def tile_picked_spconv_none_p_kernel(tc, x_words, x_scales, w1, w2, w3, offs, to
         placed = [sbuf(f"placed{d}", U, F32) for d in range(TAPS)]
         x_scale = [sbuf(f"x_scale{z}", S, U8) for z in range(PASSES)]
 
-        def load_words(z):
-            nc.sync.dma_start(word_tables[z][:], x_words[z].rearrange("p c r -> p (c r)").bitcast(I32))
+        def load_words(queue, z):
+            queue.dma_start(word_tables[z][:], x_words[z].rearrange("p c r -> p (c r)").bitcast(I32))
 
         def load_weight(d, tag):
             raw = sbuf(f"raw{d}", PASSES * PACK * N, F32, tag)
             nc.sync.dma_start(raw[:].rearrange("p (z r) -> p z r", z=PASSES), weights[d].rearrange("(z p j) m -> p z (j m)", z=PASSES, j=PACK))
             return raw
 
-        def quantize(d, raw, grouped_tag, scale_tag=None):
+        def quantize(d, raw, grouped_tag):
             grouped = sbuf(f"grouped{d}", PASSES * N * PACK, BF16, grouped_tag)
             src = raw[:].rearrange("p (z j m) -> p z m j", z=PASSES, j=PACK)
             dst = grouped[:].rearrange("p (z m j) -> p z m j", z=PASSES, j=PACK)
-            if d == 1:
-                nc.gpsimd.tensor_scalar(dst, src, 1.0, 0.0, mybir.AluOpType.mult, ADD)
-            else:
+            if d == 0:
                 nc.scalar.copy(dst, src)
+            else:
+                nc.gpsimd.tensor_scalar(dst, src, 1.0, 0.0, mybir.AluOpType.mult, ADD)
             codes = sbuf(f"w_codes{d}", PASSES * N, U32, "codes")
-            scale = sbuf(f"w_scale{d}", PASSES * N, U8, scale_tag)
+            scale = sbuf(f"w_scale{d}", PASSES * N, U8)
             nc.vector.quantize_mx(out=codes[:].bitcast(FP8X4), scales=scale[:], in_=grouped[:])
             return codes, scale
 
@@ -87,67 +87,81 @@ def tile_picked_spconv_none_p_kernel(tc, x_words, x_scales, w1, w2, w3, offs, to
         nc.sync.dma_start(scale_table[ROW0:P, :].bitcast(I32), x_scales.rearrange("z q c -> (z q) c").bitcast(I32))
         nc.sync.dma_start(picks[:], offs)
         nc.vector.memset(scale_table[0:ROW0, :].bitcast(I32), 0)
-        load_words(0)
+        load_words(nc.sync, 0)
         for tile, dram in zip(maps, (to1, to2, to3)):
             nc.sync.dma_start(tile[:], dram)
         raw0 = load_weight(0, "raw0")
-        load_words(1)
-
         zero = sbuf("zero", 1, F32)
         nc.vector.memset(zero[:], 0.0)
-        nc.vector.memset(placed[0][:], 0.0)
+        nc.scalar.copy(placed[0][:], zero[:].to_broadcast([P, U]))
         for d in range(1, TAPS):
-            nc.scalar.copy(placed[d][:], zero[:].to_broadcast([P, U]))
+            nc.gpsimd.memset(placed[d][:], 0.0)
+        load_words(nc.gpsimd, 1)
 
         picked_rows = sbuf("picked_rows", S, U8)
         nc.vector.tensor_copy(picked_rows[:], scale_table[:].indirect(picks[:]))
 
-        def move_rows(queue, z, i):
+        def move_rows(z, i):
             src = ROW0 + 16 * z + i
-            queue.dma_start(x_scale[z][4 * z + i : P : 32, :].bitcast(I32), picked_rows[src : src + 13 : 4, :].bitcast(I32))
+            nc.sync.dma_start(x_scale[z][4 * z + i : P : 32, :].bitcast(I32), picked_rows[src : src + 13 : 4, :].bitcast(I32))
 
-        moves = [(z, i) for i in range(4) for z in range(PASSES)]
-        for z, i in moves[:-1]:
-            move_rows(nc.sync, z, i)
-        move_rows(nc.gpsimd, *moves[-1])
+        for i in range(4):
+            for z in range(PASSES):
+                move_rows(z, i)
         raw1 = load_weight(1, "after_scales")
 
         words_a = sbuf("words_a", 2 * V, U32)
-        words_b = sbuf("words_b", 2 * V, U32)
+        words_b = sbuf("words_b", 2 * V, U32, "raw0")
         gather_words(0, 0, words_a[:])
-        quantized = [quantize(0, raw0, "after_first_quantise", "after_tap0")]
+        quantized = [quantize(0, raw0, "after_first_quantise")]
         raw2 = load_weight(2, "after_first_quantise")
         gather_words(1, 0, words_b[:, 0:HALF])
         gather_words(1, HALF, words_b[:, HALF:])
 
-        def multiply(first, moving, y, bank):
-            acc = psum.tile([P, y.shape[1]], F32, name=f"acc{first}", tag=bank)
+        def multiply(first, moving, bank):
+            acc = psum.tile([P, moving[0].shape[1]], F32, name=f"acc{first}", tag=bank)
             product(acc[:], quantized[first // V], first, moving, (0, 1))
-            nc.scalar.copy(y, acc[:])
+            return acc
 
-        def early_product(first, y, bank):
-            end = first + y.shape[1]
-            multiply(first, (words_a[:, first:end], words_b[:, first:end]), y, bank)
+        def early_product(first, count, bank):
+            return multiply(first, (words_a[:, first : first + count], words_b[:, first : first + count]), bank)
 
-        ys = [sbuf(f"y{d}", V, F32) for d in range(TAPS)]
-        late = [words_a[:, 0:V], words_b[:, CHUNK : CHUNK + V]]
-        early_product(0, ys[0][:, 0:CHUNK], "chain")
-        for k in range(4):
-            at = (k + 1) * CHUNK
-            if k == 3:
-                quantized.append(quantize(1, raw1, None))
-            early_product(at, ys[at // V][:, at % V : at % V + CHUNK], "chain")
-            scatter(0, k * CHUNK, ys[0][:, k * CHUNK : at])
-            half, z = divmod(k, PASSES)
-            gather_words(z, 2 * V + half * HALF, late[z][:, half * HALF : (half + 1) * HALF])
+        def leave(name, sums, tag=None):
+            y = sbuf(name, sums.shape[1], F32, tag)
+            nc.scalar.copy(y[:], sums)
+            return y
 
-        early_product(V + HALF, ys[1][:, HALF:V], "rest")
-        early_product(V + CHUNK, ys[1][:, CHUNK:HALF], "chain")
-        scatter(1, 0, ys[1][:, 0:CHUNK])
-        quantized.append(quantize(2, raw2, "after_tap0"))
-        scatter(1, CHUNK, ys[1][:, CHUNK:V])
-        multiply(2 * V, late, ys[2][:], "last")
-        scatter(2, 0, ys[2][:])
+        late = {(0, 0): words_a[:, 0:256], (1, 0): words_b[:, 256:512], (0, 1): words_a[:, 384:640], (1, 1): words_b[:, 512:768]}
+
+        def gather_late(z, half):
+            gather_words(z, 2 * V + half * HALF, late[z, half])
+
+        y0_a = leave("y0_a", early_product(0, HALF, "chain")[:, 0:192])
+        y0_b = leave("y0_b", early_product(192, CHUNK, "chain")[:])
+        scatter(0, 0, y0_a[:])
+        gather_late(0, 0)
+        acc_c = early_product(HALF, HALF, "chain")
+        scatter(0, 192, y0_b[:])
+        gather_late(1, 0)
+        quantized.append(quantize(1, raw1, "grouped_late"))
+        y0_c = leave("y0_c", acc_c[:, 64:], "after_scales")
+        y1_first = leave("y1_first", early_product(V, CHUNK, "chain")[:])
+        scatter(0, 320, y0_c[:])
+        gather_late(0, 1)
+        acc_rest = early_product(V + HALF, HALF, "rest")
+        acc_next = early_product(V + CHUNK, CHUNK, "chain")
+        scatter(1, 0, y1_first[:])
+        gather_late(1, 1)
+        quantized.append(quantize(2, raw2, "grouped_late"))
+        y1_rest = sbuf("y1_rest", V - CHUNK, F32, "after_first_quantise")
+        nc.scalar.copy(y1_rest[:, CHUNK:], acc_rest[:])
+        nc.scalar.copy(y1_rest[:, 0:CHUNK], acc_next[:])
+        scatter(1, CHUNK, y1_rest[:])
+        y2 = sbuf("y2", V, F32)
+        for half in range(2):
+            acc = multiply(2 * V + half * HALF, (late[0, half], late[1, half]), f"last{half}")
+            nc.scalar.copy(y2[:, half * HALF : (half + 1) * HALF], acc[:])
+        scatter(2, 0, y2[:])
 
         for c in range(U // STORE_COLS):
             cols = slice(c * STORE_COLS, (c + 1) * STORE_COLS)

@@ -86,16 +86,16 @@ def tile_picked_spconv_none_p_kernel(tc, x_words, x_scales, w1, w2, w3, offs, to
 
         nc.sync.dma_start(scale_table[ROW0:P, :].bitcast(I32), x_scales.rearrange("z q c -> (z q) c").bitcast(I32))
         nc.sync.dma_start(picks[:], offs)
-        nc.vector.memset(scale_table[0:ROW0, :].bitcast(I32), 0)
+        nc.gpsimd.memset(scale_table[0:ROW0, :].bitcast(I32), 0)
         load_words(nc.sync, 0)
         for tile, dram in zip(maps, (to1, to2, to3)):
             nc.sync.dma_start(tile[:], dram)
         raw0 = load_weight(0, "raw0")
         zero = sbuf("zero", 1, F32)
-        nc.vector.memset(zero[:], 0.0)
-        nc.scalar.copy(placed[0][:], zero[:].to_broadcast([P, U]))
+        nc.gpsimd.memset(zero[:], 0.0)
+        nc.gpsimd.memset(placed[0][:], 0.0)
         for d in range(1, TAPS):
-            nc.gpsimd.memset(placed[d][:], 0.0)
+            nc.scalar.copy(placed[d][:], zero[:].to_broadcast([P, U]))
         load_words(nc.gpsimd, 1)
 
         picked_rows = sbuf("picked_rows", S, U8)

@@ -40,8 +40,8 @@ def tile_picked_spconv_none_p_kernel(tc, x_words, x_scales, w1, w2, w3, offs, to
         placed = [sbuf(f"placed{d}", U, F32) for d in range(TAPS)]
         x_scale = [sbuf(f"x_scale{z}", S, U8) for z in range(PASSES)]
 
-        def load_words(queue, z):
-            queue.dma_start(word_tables[z][:], x_words[z].rearrange("p c r -> p (c r)").bitcast(I32))
+        def load_words(z):
+            nc.sync.dma_start(word_tables[z][:], x_words[z].rearrange("p c r -> p (c r)").bitcast(I32))
 
         def load_weight(d, tag):
             raw = sbuf(f"raw{d}", PASSES * PACK * N, F32, tag)
@@ -52,10 +52,11 @@ def tile_picked_spconv_none_p_kernel(tc, x_words, x_scales, w1, w2, w3, offs, to
             grouped = sbuf(f"grouped{d}", PASSES * N * PACK, BF16, grouped_tag)
             src = raw[:].rearrange("p (z j m) -> p z m j", z=PASSES, j=PACK)
             dst = grouped[:].rearrange("p (z m j) -> p z m j", z=PASSES, j=PACK)
-            if d == 0:
-                nc.scalar.copy(dst, src)
-            else:
-                nc.gpsimd.tensor_scalar(dst, src, 1.0, 0.0, mybir.AluOpType.mult, ADD)
+            on_scalar = PASSES - d
+            if on_scalar > 0:
+                nc.scalar.copy(dst[:, :on_scalar], src[:, :on_scalar])
+            if on_scalar < PASSES:
+                nc.gpsimd.tensor_scalar(dst[:, on_scalar:], src[:, on_scalar:], 1.0, 0.0, mybir.AluOpType.mult, ADD)
             codes = sbuf(f"w_codes{d}", PASSES * N, U32, "codes")
             scale = sbuf(f"w_scale{d}", PASSES * N, U8)
             nc.vector.quantize_mx(out=codes[:].bitcast(FP8X4), scales=scale[:], in_=grouped[:])
@@ -86,31 +87,33 @@ def tile_picked_spconv_none_p_kernel(tc, x_words, x_scales, w1, w2, w3, offs, to
 
         nc.sync.dma_start(scale_table[ROW0:P, :].bitcast(I32), x_scales.rearrange("z q c -> (z q) c").bitcast(I32))
         nc.sync.dma_start(picks[:], offs)
-        nc.gpsimd.memset(scale_table[0:ROW0, :].bitcast(I32), 0)
-        load_words(nc.sync, 0)
+        nc.vector.memset(scale_table[0:ROW0, :].bitcast(I32), 0)
+        load_words(0)
         for tile, dram in zip(maps, (to1, to2, to3)):
             nc.sync.dma_start(tile[:], dram)
         raw0 = load_weight(0, "raw0")
+        load_words(1)
+
         zero = sbuf("zero", 1, F32)
-        nc.gpsimd.memset(zero[:], 0.0)
-        nc.gpsimd.memset(placed[0][:], 0.0)
+        nc.vector.memset(zero[:], 0.0)
+        nc.vector.memset(placed[0][:], 0.0)
         for d in range(1, TAPS):
             nc.scalar.copy(placed[d][:], zero[:].to_broadcast([P, U]))
-        load_words(nc.gpsimd, 1)
 
         picked_rows = sbuf("picked_rows", S, U8)
         nc.vector.tensor_copy(picked_rows[:], scale_table[:].indirect(picks[:]))
 
-        def move_rows(z, i):
+        def move_rows(queue, z, i):
             src = ROW0 + 16 * z + i
-            nc.sync.dma_start(x_scale[z][4 * z + i : P : 32, :].bitcast(I32), picked_rows[src : src + 13 : 4, :].bitcast(I32))
+            queue.dma_start(x_scale[z][4 * z + i : P : 32, :].bitcast(I32), picked_rows[src : src + 13 : 4, :].bitcast(I32))
 
-        for i in range(4):
-            for z in range(PASSES):
-                move_rows(z, i)
+        moves = [(z, i) for i in range(4) for z in range(PASSES)]
+        for z, i in moves[:-1]:
+            move_rows(nc.sync, z, i)
+        move_rows(nc.gpsimd, *moves[-1])
         raw1 = load_weight(1, "after_scales")
 
-        words_a = sbuf("words_a", 2 * V, U32)
+        words_a = sbuf("words_a", 2 * V + HALF, U32)
         words_b = sbuf("words_b", 2 * V, U32, "raw0")
         gather_words(0, 0, words_a[:])
         quantized = [quantize(0, raw0, "after_first_quantise")]
@@ -131,35 +134,29 @@ def tile_picked_spconv_none_p_kernel(tc, x_words, x_scales, w1, w2, w3, offs, to
             nc.scalar.copy(y[:], sums)
             return y
 
-        late = {(0, 0): words_a[:, 0:256], (1, 0): words_b[:, 256:512], (0, 1): words_a[:, 384:640], (1, 1): words_b[:, 512:768]}
+        late_1a, late_0b, late_1b = words_b[:, 256:512], words_a[:, 384:640], words_b[:, 512:768]
 
-        def gather_late(z, half):
-            gather_words(z, 2 * V + half * HALF, late[z, half])
-
-        y0_a = leave("y0_a", early_product(0, HALF, "chain")[:, 0:192])
-        y0_b = leave("y0_b", early_product(192, CHUNK, "chain")[:])
+        y0_a = leave("y0_a", early_product(0, HALF, "chain")[:])
+        acc_b = early_product(HALF, HALF, "chain")
         scatter(0, 0, y0_a[:])
-        gather_late(0, 0)
-        acc_c = early_product(HALF, HALF, "chain")
-        scatter(0, 192, y0_b[:])
-        gather_late(1, 0)
+        gather_words(1, 2 * V, late_1a)
         quantized.append(quantize(1, raw1, "grouped_late"))
-        y0_c = leave("y0_c", acc_c[:, 64:], "after_scales")
+        y0_b = leave("y0_b", acc_b[:], "after_scales")
         y1_first = leave("y1_first", early_product(V, CHUNK, "chain")[:])
-        scatter(0, 320, y0_c[:])
-        gather_late(0, 1)
+        scatter(0, HALF, y0_b[:])
+        gather_words(0, 2 * V + HALF, late_0b)
         acc_rest = early_product(V + HALF, HALF, "rest")
         acc_next = early_product(V + CHUNK, CHUNK, "chain")
         scatter(1, 0, y1_first[:])
-        gather_late(1, 1)
+        gather_words(1, 2 * V + HALF, late_1b)
         quantized.append(quantize(2, raw2, "grouped_late"))
         y1_rest = sbuf("y1_rest", V - CHUNK, F32, "after_first_quantise")
         nc.scalar.copy(y1_rest[:, CHUNK:], acc_rest[:])
         nc.scalar.copy(y1_rest[:, 0:CHUNK], acc_next[:])
         scatter(1, CHUNK, y1_rest[:])
         y2 = sbuf("y2", V, F32)
-        for half in range(2):
-            acc = multiply(2 * V + half * HALF, (late[0, half], late[1, half]), f"last{half}")
+        for half, moving in enumerate(((words_a[:, 2 * V :], late_1a), (late_0b, late_1b))):
+            acc = multiply(2 * V + half * HALF, moving, f"last{half}")
             nc.scalar.copy(y2[:, half * HALF : (half + 1) * HALF], acc[:])
         scatter(2, 0, y2[:])
 

@@ -10,7 +10,12 @@ PASSES = K // (P * PACK)
 HALF = V // 2
 CHUNK = 128
 ROW0 = P - 16 * PASSES
+EARLY = V + HALF
 STORE_COLS = 256
+AT_RAW2 = 0
+AT_RAW0 = 3072
+AT_SCALES = 4096
+AT_RAW1 = 6144
 FLOPS = 2 * K * N * S
 
 F32 = mybir.dt.float32
@@ -21,6 +26,8 @@ U16 = mybir.dt.uint16
 U8 = mybir.dt.uint8
 FP8X4 = mybir.dt.float8_e4m3fn_x4
 ADD = mybir.AluOpType.add
+MULT = mybir.AluOpType.mult
+COPY = mybir.ActivationFunctionType.Copy
 
 
 def tile_picked_spconv_none_p_kernel(tc, x_words, x_scales, w1, w2, w3, offs, to1, to2, to3, out):
@@ -28,36 +35,38 @@ def tile_picked_spconv_none_p_kernel(tc, x_words, x_scales, w1, w2, w3, offs, to
     weights = (w1, w2, w3)
     with ExitStack() as ctx:
         keep = ctx.enter_context(tc.tile_pool(name="keep", bufs=1))
+        reuse = ctx.enter_context(tc.tile_pool(name="reuse", bufs=1))
         psum = ctx.enter_context(tc.psum_pool(name="psum", bufs=1))
 
         def sbuf(name, cols, dtype, tag=None):
             return keep.tile([P, cols], dtype, name=name, tag=tag or name, align_bytes=64)
 
+        def placed_at(name, cols, dtype, offset):
+            return reuse.tile([P, cols], dtype, name=name, align_bytes=64, offset=offset)
+
         picks = keep.tile([P, S // 16], U16, name="picks")
         maps = [keep.tile([P, V // 16], U16, name=f"map{d}") for d in range(TAPS)]
-        scale_table = sbuf("scale_table", T, U8, "after_scales")
+        scale_table = sbuf("scale_table", T, U8)
         word_tables = [sbuf(f"word_table{z}", T, I32) for z in range(PASSES)]
         placed = [sbuf(f"placed{d}", U, F32) for d in range(TAPS)]
-        x_scale = [sbuf(f"x_scale{z}", S, U8) for z in range(PASSES)]
 
         def load_words(z):
             nc.sync.dma_start(word_tables[z][:], x_words[z].rearrange("p c r -> p (c r)").bitcast(I32))
 
-        def load_weight(d, tag):
-            raw = sbuf(f"raw{d}", PASSES * PACK * N, F32, tag)
-            nc.sync.dma_start(raw[:].rearrange("p (z r) -> p z r", z=PASSES), weights[d].rearrange("(z p j) m -> p z (j m)", z=PASSES, j=PACK))
-            return raw
+        def load_weight(queue, d, raw):
+            queue.dma_start(raw[:].rearrange("p (z r) -> p z r", z=PASSES), weights[d].rearrange("(z p j) m -> p z (j m)", z=PASSES, j=PACK))
 
-        def quantize(d, raw, grouped_tag):
-            grouped = sbuf(f"grouped{d}", PASSES * N * PACK, BF16, grouped_tag)
+        def regroup(d, raw, grouped):
             src = raw[:].rearrange("p (z j m) -> p z m j", z=PASSES, j=PACK)
             dst = grouped[:].rearrange("p (z m j) -> p z m j", z=PASSES, j=PACK)
-            on_scalar = PASSES - d
-            if on_scalar > 0:
-                nc.scalar.copy(dst[:, :on_scalar], src[:, :on_scalar])
-            if on_scalar < PASSES:
-                nc.gpsimd.tensor_scalar(dst[:, on_scalar:], src[:, on_scalar:], 1.0, 0.0, mybir.AluOpType.mult, ADD)
-            codes = sbuf(f"w_codes{d}", PASSES * N, U32, "codes")
+            if d == 0:
+                nc.scalar.copy(dst, src)
+            else:
+                nc.gpsimd.tensor_scalar(dst, src, 1.0, 0.0, MULT, ADD)
+            return grouped
+
+        def quantize(d, grouped):
+            codes = sbuf(f"w_codes{d}", PASSES * N, U32)
             scale = sbuf(f"w_scale{d}", PASSES * N, U8)
             nc.vector.quantize_mx(out=codes[:].bitcast(FP8X4), scales=scale[:], in_=grouped[:])
             return codes, scale
@@ -65,105 +74,129 @@ def tile_picked_spconv_none_p_kernel(tc, x_words, x_scales, w1, w2, w3, offs, to
         def gather_words(z, first, piece):
             count = piece.shape[1]
             nc.vector.tensor_copy(piece, word_tables[z][:].bitcast(U32).indirect(picks[:, first // 16 : (first + count) // 16]))
-            return piece
 
-        def product(acc, quantized, first, moving, passes):
-            codes, scale = quantized
-            count = acc.shape[1]
-            for z in passes:
-                nc.tensor.matmul_mx(
-                    out=acc,
-                    lhsT=codes[:, z * N : (z + 1) * N].bitcast(FP8X4),
-                    lhsT_scale=scale[:, z * N : (z + 1) * N],
-                    rhs=moving[z].bitcast(FP8X4),
-                    rhs_scale=x_scale[z][4 * z :, first : first + count],
-                    start=(z == passes[0]),
-                    stop=(z == passes[-1]),
-                )
+        def window(d, first, count):
+            return placed[d][:].indirect(maps[d][:, first // 16 : (first + count) // 16])
 
-        def scatter(d, first, values):
-            count = values.shape[1]
-            nc.vector.tensor_copy(placed[d][:].indirect(maps[d][:, first // 16 : (first + count) // 16]), values)
-
+        raw0 = placed_at("raw0", PASSES * PACK * N, F32, AT_RAW0)
         nc.sync.dma_start(scale_table[ROW0:P, :].bitcast(I32), x_scales.rearrange("z q c -> (z q) c").bitcast(I32))
         nc.sync.dma_start(picks[:], offs)
         nc.vector.memset(scale_table[0:ROW0, :].bitcast(I32), 0)
-        load_words(0)
         for tile, dram in zip(maps, (to1, to2, to3)):
             nc.sync.dma_start(tile[:], dram)
-        raw0 = load_weight(0, "raw0")
+        load_weight(nc.sync, 0, raw0)
+        load_words(0)
         load_words(1)
 
         zero = sbuf("zero", 1, F32)
         nc.vector.memset(zero[:], 0.0)
-        nc.vector.memset(placed[0][:], 0.0)
-        for d in range(1, TAPS):
-            nc.scalar.copy(placed[d][:], zero[:].to_broadcast([P, U]))
+        nc.vector.memset(placed[1][:], 0.0)
+        for d in (0, 2):
+            nc.scalar.activation(placed[d][:], zero[:].to_broadcast([P, U]), COPY)
 
-        picked_rows = sbuf("picked_rows", S, U8)
-        nc.vector.tensor_copy(picked_rows[:], scale_table[:].indirect(picks[:]))
+        def pick_scales(name, first, count):
+            rows = sbuf(name, count, U8)
+            nc.vector.tensor_copy(rows[:], scale_table[:].indirect(picks[:, first // 16 : (first + count) // 16]))
+            return rows
 
-        def move_rows(queue, z, i):
-            src = ROW0 + 16 * z + i
-            queue.dma_start(x_scale[z][4 * z + i : P : 32, :].bitcast(I32), picked_rows[src : src + 13 : 4, :].bitcast(I32))
+        def move_rows(rows, planes):
+            moves = [(z, i) for i in range(4) for z in range(PASSES)]
+            for z, i in moves:
+                queue = nc.gpsimd if (z, i) == moves[-1] else nc.sync
+                src = ROW0 + 16 * z + i
+                queue.dma_start(planes[z][4 * z + i : P : 32, :].bitcast(I32), rows[src : src + 13 : 4, :].bitcast(I32))
 
-        moves = [(z, i) for i in range(4) for z in range(PASSES)]
-        for z, i in moves[:-1]:
-            move_rows(nc.sync, z, i)
-        move_rows(nc.gpsimd, *moves[-1])
-        raw1 = load_weight(1, "after_scales")
+        rows_early = pick_scales("rows_early", 0, V)
+        rows_late = pick_scales("rows_late", V, S - V)
+        scale_early = [sbuf(f"scale_early{z}", V, U8) for z in range(PASSES)]
+        move_rows(rows_early, scale_early)
+        quantized = [quantize(0, regroup(0, raw0, sbuf("grouped0", PASSES * N * PACK, BF16)))]
 
-        words_a = sbuf("words_a", 2 * V + HALF, U32)
-        words_b = sbuf("words_b", 2 * V, U32, "raw0")
-        gather_words(0, 0, words_a[:])
-        quantized = [quantize(0, raw0, "after_first_quantise")]
-        raw2 = load_weight(2, "after_first_quantise")
-        gather_words(1, 0, words_b[:, 0:HALF])
-        gather_words(1, HALF, words_b[:, HALF:])
+        raw1 = placed_at("raw1", PASSES * PACK * N, F32, AT_RAW1)
+        load_weight(nc.gpsimd, 1, raw1)
+        raw2 = placed_at("raw2", PASSES * PACK * N, F32, AT_RAW2)
+        load_weight(nc.sync, 2, raw2)
+        scale_late = [placed_at(f"scale_late{z}", S - V, U8, AT_SCALES + z * (S - V)) for z in range(PASSES)]
+        move_rows(rows_late, scale_late)
 
-        def multiply(first, moving, bank):
-            acc = psum.tile([P, moving[0].shape[1]], F32, name=f"acc{first}", tag=bank)
-            product(acc[:], quantized[first // V], first, moving, (0, 1))
+        def x_scale(z, first, count):
+            if first < V:
+                return scale_early[z][4 * z :, first : first + count]
+            return scale_late[z][4 * z :, first - V : first - V + count]
+
+        def multiply(first, moving):
+            codes, scale = quantized[first // V]
+            count = moving[0].shape[1]
+            acc = psum.tile([P, count], F32, name=f"acc{first}")
+            for z in range(PASSES):
+                nc.tensor.matmul_mx(
+                    out=acc[:],
+                    lhsT=codes[:, z * N : (z + 1) * N].bitcast(FP8X4),
+                    lhsT_scale=scale[:, z * N : (z + 1) * N],
+                    rhs=moving[z].bitcast(FP8X4),
+                    rhs_scale=x_scale(z, first, count),
+                    start=(z == 0),
+                    stop=(z == PASSES - 1),
+                )
             return acc
 
-        def early_product(first, count, bank):
-            return multiply(first, (words_a[:, first : first + count], words_b[:, first : first + count]), bank)
-
-        def leave(name, sums, tag=None):
-            y = sbuf(name, sums.shape[1], F32, tag)
-            nc.scalar.copy(y[:], sums)
+        def leave(first, moving, y=None):
+            acc = multiply(first, moving)
+            if y is None:
+                y = sbuf(f"y{first}", acc.shape[1], F32)[:]
+            nc.scalar.copy(y, acc[:])
             return y
 
-        late_1a, late_0b, late_1b = words_b[:, 256:512], words_a[:, 384:640], words_b[:, 512:768]
+        def scatter_on_scalar(first, y):
+            nc.scalar.activation(window(first // V, first % V, y.shape[1]), y, COPY)
 
-        y0_a = leave("y0_a", early_product(0, HALF, "chain")[:])
-        acc_b = early_product(HALF, HALF, "chain")
-        scatter(0, 0, y0_a[:])
-        gather_words(1, 2 * V, late_1a)
-        quantized.append(quantize(1, raw1, "grouped_late"))
-        y0_b = leave("y0_b", acc_b[:], "after_scales")
-        y1_first = leave("y1_first", early_product(V, CHUNK, "chain")[:])
-        scatter(0, HALF, y0_b[:])
-        gather_words(0, 2 * V + HALF, late_0b)
-        acc_rest = early_product(V + HALF, HALF, "rest")
-        acc_next = early_product(V + CHUNK, CHUNK, "chain")
-        scatter(1, 0, y1_first[:])
-        gather_words(1, 2 * V + HALF, late_1b)
-        quantized.append(quantize(2, raw2, "grouped_late"))
-        y1_rest = sbuf("y1_rest", V - CHUNK, F32, "after_first_quantise")
-        nc.scalar.copy(y1_rest[:, CHUNK:], acc_rest[:])
-        nc.scalar.copy(y1_rest[:, 0:CHUNK], acc_next[:])
-        scatter(1, CHUNK, y1_rest[:])
-        y2 = sbuf("y2", V, F32)
-        for half, moving in enumerate(((words_a[:, 2 * V :], late_1a), (late_0b, late_1b))):
-            acc = multiply(2 * V + half * HALF, moving, f"last{half}")
-            nc.scalar.copy(y2[:, half * HALF : (half + 1) * HALF], acc[:])
-        scatter(2, 0, y2[:])
+        def scatter_on_vector(first, y):
+            nc.vector.tensor_copy(window(first // V, first % V, y.shape[1]), y)
 
+        a_early = sbuf("a_early", EARLY, U32)
+        b_first = sbuf("b_first", CHUNK, U32, "after_first_product")
+        b_early = sbuf("b_early", 2 * V - CHUNK, U32)
+        gather_words(0, 0, a_early[:])
+        gather_words(1, 0, b_first[:])
+        gather_words(1, CHUNK, b_early[:, 0 : V - CHUNK])
+        gather_words(1, V, b_early[:, V - CHUNK :])
+
+        def early(first, count):
+            return a_early[:, first : first + count], b_early[:, first - CHUNK : first - CHUNK + count]
+
+        scatter_on_scalar(0, leave(0, (a_early[:, 0:CHUNK], b_first[:])))
+        y_second = leave(CHUNK, early(CHUNK, CHUNK))
+        y_third = leave(HALF, early(HALF, HALF))
+        scatter_on_scalar(CHUNK, y_second)
+
+        scatter_on_scalar(HALF, y_third)
+
+        a_mid = sbuf("a_mid", HALF, U32, "after_first_product")
+        gather_words(0, EARLY, a_mid[:])
+        quantized.append(quantize(1, regroup(1, raw1, sbuf("grouped1", PASSES * N * PACK, BF16, "grouped_late"))))
+        scatter_on_scalar(V, leave(V, early(V, CHUNK)))
+        late = placed_at("late", 3 * HALF, U32, AT_RAW1)
+        a_late, b_late, a_last = (late[:, j * HALF : (j + 1) * HALF] for j in range(3))
+        gather_words(0, 2 * V, a_late)
+        gather_words(1, 2 * V, b_late)
+        gather_words(0, 2 * V + HALF, a_last)
+        quantized.append(quantize(2, regroup(2, raw2, sbuf("grouped2", PASSES * N * PACK, BF16, "grouped_late"))))
+        b_last = placed_at("b_last", HALF, U32, AT_RAW2)
+        gather_words(1, 2 * V + HALF, b_last[:])
+
+        y1_rest = placed_at("y1_rest", V - CHUNK, F32, AT_RAW2 + 1024)
+        leave(V + CHUNK, early(V + CHUNK, CHUNK), y1_rest[:, 0:CHUNK])
+        leave(EARLY, (a_mid[:], b_early[:, EARLY - CHUNK :]), y1_rest[:, CHUNK:])
+        y2_a = leave(2 * V, (a_late, b_late))
+        y2_b = leave(2 * V + HALF, (a_last, b_last[:]))
+        scatter_on_vector(V + CHUNK, y1_rest[:])
+        scatter_on_scalar(2 * V, y2_a)
+        scatter_on_scalar(2 * V + HALF, y2_b)
+
+        pair = sbuf("pair", U, F32)
+        nc.vector.tensor_tensor(pair[:], placed[0][:], placed[1][:], ADD)
         for c in range(U // STORE_COLS):
             cols = slice(c * STORE_COLS, (c + 1) * STORE_COLS)
-            pair = sbuf(f"pair{c}", STORE_COLS, F32)
-            nc.gpsimd.tensor_tensor(pair[:], placed[0][:, cols], placed[1][:, cols], ADD)
             total = sbuf(f"total{c}", STORE_COLS, F32)
-            nc.vector.tensor_tensor(total[:], pair[:], placed[2][:, cols], ADD)
+            nc.vector.tensor_tensor(total[:], pair[:, cols], placed[2][:, cols], ADD)
             nc.sync.dma_start(out[:, cols], total[:])

@@ -10,7 +10,7 @@ PASSES = K // (P * PACK)
 HALF = V // 2
 CHUNK = 128
 ROW0 = P - 16 * PASSES
-EARLY = V + HALF
+EARLY = V + CHUNK
 STORE_COLS = 256
 AT_RAW2 = 0
 AT_RAW0 = 3072
@@ -128,30 +128,28 @@ def tile_picked_spconv_none_p_kernel(tc, x_words, x_scales, w1, w2, w3, offs, to
             codes, scale = quantized[first // V]
             count = moving[0].shape[1]
             acc = psum.tile([P, count], F32, name=f"acc{first}")
-            for z in range(PASSES):
+            spans = [(0, CHUNK), (CHUNK, count)] if count == V - CHUNK else [(0, count)]
+            steps = [(z, span) for z in range(PASSES) for span in spans]
+            for z, (lo, hi) in steps:
                 nc.tensor.matmul_mx(
-                    out=acc[:],
+                    out=acc[:, lo:hi],
                     lhsT=codes[:, z * N : (z + 1) * N].bitcast(FP8X4),
                     lhsT_scale=scale[:, z * N : (z + 1) * N],
-                    rhs=moving[z].bitcast(FP8X4),
-                    rhs_scale=x_scale(z, first, count),
-                    start=(z == 0),
-                    stop=(z == PASSES - 1),
+                    rhs=moving[z][:, lo:hi].bitcast(FP8X4),
+                    rhs_scale=x_scale(z, first + lo, hi - lo),
+                    start=((z, (lo, hi)) == steps[0]),
+                    stop=((z, (lo, hi)) == steps[-1]),
                 )
             return acc
 
-        def leave(first, moving, y=None):
+        def leave(first, moving):
             acc = multiply(first, moving)
-            if y is None:
-                y = sbuf(f"y{first}", acc.shape[1], F32)[:]
-            nc.scalar.copy(y, acc[:])
+            y = sbuf(f"y{first}", acc.shape[1], F32)
+            nc.scalar.copy(y[:], acc[:])
             return y
 
         def scatter_on_scalar(first, y):
-            nc.scalar.activation(window(first // V, first % V, y.shape[1]), y, COPY)
-
-        def scatter_on_vector(first, y):
-            nc.vector.tensor_copy(window(first // V, first % V, y.shape[1]), y)
+            nc.scalar.activation(window(first // V, first % V, y.shape[1]), y[:], COPY)
 
         a_early = sbuf("a_early", EARLY, U32)
         b_first = sbuf("b_first", CHUNK, U32, "after_first_product")
@@ -165,36 +163,32 @@ def tile_picked_spconv_none_p_kernel(tc, x_words, x_scales, w1, w2, w3, offs, to
             return a_early[:, first : first + count], b_early[:, first - CHUNK : first - CHUNK + count]
 
         scatter_on_scalar(0, leave(0, (a_early[:, 0:CHUNK], b_first[:])))
-        y_second = leave(CHUNK, early(CHUNK, CHUNK))
-        y_third = leave(HALF, early(HALF, HALF))
-        scatter_on_scalar(CHUNK, y_second)
+        scatter_on_scalar(CHUNK, leave(CHUNK, early(CHUNK, V - CHUNK)))
 
-        scatter_on_scalar(HALF, y_third)
-
-        a_mid = sbuf("a_mid", HALF, U32, "after_first_product")
+        a_mid = sbuf("a_mid", 2 * V - EARLY, U32, "after_first_product")
         gather_words(0, EARLY, a_mid[:])
         quantized.append(quantize(1, regroup(1, raw1, sbuf("grouped1", PASSES * N * PACK, BF16, "grouped_late"))))
-        scatter_on_scalar(V, leave(V, early(V, CHUNK)))
+        y1_first = leave(V, early(V, CHUNK))
         late = placed_at("late", 3 * HALF, U32, AT_RAW1)
-        a_late, b_late, a_last = (late[:, j * HALF : (j + 1) * HALF] for j in range(3))
+        a_late, b_late = late[:, 0:V], late[:, V:]
         gather_words(0, 2 * V, a_late)
         gather_words(1, 2 * V, b_late)
-        gather_words(0, 2 * V + HALF, a_last)
         quantized.append(quantize(2, regroup(2, raw2, sbuf("grouped2", PASSES * N * PACK, BF16, "grouped_late"))))
+        y1_rest = placed_at("y1_rest", V - CHUNK, F32, AT_RAW2 + 1024)
+        nc.vector.tensor_copy(y1_rest[:], multiply(EARLY, (a_mid[:], b_early[:, EARLY - CHUNK :]))[:])
         b_last = placed_at("b_last", HALF, U32, AT_RAW2)
         gather_words(1, 2 * V + HALF, b_last[:])
 
-        y1_rest = placed_at("y1_rest", V - CHUNK, F32, AT_RAW2 + 1024)
-        leave(V + CHUNK, early(V + CHUNK, CHUNK), y1_rest[:, 0:CHUNK])
-        leave(EARLY, (a_mid[:], b_early[:, EARLY - CHUNK :]), y1_rest[:, CHUNK:])
-        y2_a = leave(2 * V, (a_late, b_late))
-        y2_b = leave(2 * V + HALF, (a_last, b_last[:]))
-        scatter_on_vector(V + CHUNK, y1_rest[:])
+        y2_a = leave(2 * V, (a_late[:, 0:HALF], b_late))
+        scatter_on_scalar(V, y1_first)
+        nc.vector.tensor_copy(window(1, CHUNK, V - CHUNK), y1_rest[:])
+        y2_b = leave(2 * V + HALF, (a_late[:, HALF:], b_last[:]))
         scatter_on_scalar(2 * V, y2_a)
         scatter_on_scalar(2 * V + HALF, y2_b)
 
         pair = sbuf("pair", U, F32)
-        nc.vector.tensor_tensor(pair[:], placed[0][:], placed[1][:], ADD)
+        for half in (slice(0, U // 2), slice(U // 2, U)):
+            nc.vector.tensor_tensor(pair[:, half], placed[0][:, half], placed[1][:, half], ADD)
         for c in range(U // STORE_COLS):
             cols = slice(c * STORE_COLS, (c + 1) * STORE_COLS)
             total = sbuf(f"total{c}", STORE_COLS, F32)

@@ -10,12 +10,11 @@ PASSES = K // (P * PACK)
 HALF = V // 2
 CHUNK = 128
 ROW0 = P - 16 * PASSES
-EARLY = V + CHUNK
+EARLY = 2 * V + HALF
 STORE_COLS = 256
 AT_RAW2 = 0
-AT_RAW0 = 3072
-AT_SCALES = 4096
-AT_RAW1 = 6144
+AT_FIRST = 5120
+AT_LATE = 8192
 FLOPS = 2 * K * N * S
 
 F32 = mybir.dt.float32
@@ -59,7 +58,7 @@ def tile_picked_spconv_none_p_kernel(tc, x_words, x_scales, w1, w2, w3, offs, to
         def regroup(d, raw, grouped):
             src = raw[:].rearrange("p (z j m) -> p z m j", z=PASSES, j=PACK)
             dst = grouped[:].rearrange("p (z m j) -> p z m j", z=PASSES, j=PACK)
-            if d == 0:
+            if d < 2:
                 nc.scalar.copy(dst, src)
             else:
                 nc.gpsimd.tensor_scalar(dst, src, 1.0, 0.0, MULT, ADD)
@@ -78,14 +77,15 @@ def tile_picked_spconv_none_p_kernel(tc, x_words, x_scales, w1, w2, w3, offs, to
         def window(d, first, count):
             return placed[d][:].indirect(maps[d][:, first // 16 : (first + count) // 16])
 
-        raw0 = placed_at("raw0", PASSES * PACK * N, F32, AT_RAW0)
+        raws = [sbuf(f"raw{d}", PASSES * PACK * N, F32) for d in range(2)]
         nc.sync.dma_start(scale_table[ROW0:P, :].bitcast(I32), x_scales.rearrange("z q c -> (z q) c").bitcast(I32))
         nc.sync.dma_start(picks[:], offs)
         nc.vector.memset(scale_table[0:ROW0, :].bitcast(I32), 0)
         for tile, dram in zip(maps, (to1, to2, to3)):
             nc.sync.dma_start(tile[:], dram)
-        load_weight(nc.sync, 0, raw0)
+        load_weight(nc.sync, 0, raws[0])
         load_words(0)
+        load_weight(nc.sync, 1, raws[1])
         load_words(1)
 
         zero = sbuf("zero", 1, F32)
@@ -94,40 +94,26 @@ def tile_picked_spconv_none_p_kernel(tc, x_words, x_scales, w1, w2, w3, offs, to
         for d in (0, 2):
             nc.scalar.activation(placed[d][:], zero[:].to_broadcast([P, U]), COPY)
 
-        def pick_scales(name, first, count):
-            rows = sbuf(name, count, U8)
-            nc.vector.tensor_copy(rows[:], scale_table[:].indirect(picks[:, first // 16 : (first + count) // 16]))
-            return rows
-
-        def move_rows(rows, planes):
-            moves = [(z, i) for i in range(4) for z in range(PASSES)]
-            for z, i in moves:
-                queue = nc.gpsimd if (z, i) == moves[-1] else nc.sync
-                src = ROW0 + 16 * z + i
-                queue.dma_start(planes[z][4 * z + i : P : 32, :].bitcast(I32), rows[src : src + 13 : 4, :].bitcast(I32))
-
-        rows_early = pick_scales("rows_early", 0, V)
-        rows_late = pick_scales("rows_late", V, S - V)
-        scale_early = [sbuf(f"scale_early{z}", V, U8) for z in range(PASSES)]
-        move_rows(rows_early, scale_early)
-        quantized = [quantize(0, regroup(0, raw0, sbuf("grouped0", PASSES * N * PACK, BF16)))]
-
-        raw1 = placed_at("raw1", PASSES * PACK * N, F32, AT_RAW1)
-        load_weight(nc.gpsimd, 1, raw1)
-        raw2 = placed_at("raw2", PASSES * PACK * N, F32, AT_RAW2)
-        load_weight(nc.sync, 2, raw2)
-        scale_late = [placed_at(f"scale_late{z}", S - V, U8, AT_SCALES + z * (S - V)) for z in range(PASSES)]
-        move_rows(rows_late, scale_late)
+        picked_rows = sbuf("picked_rows", S, U8)
+        nc.vector.tensor_copy(picked_rows[:], scale_table[:].indirect(picks[:]))
+        planes = [sbuf(f"plane{z}", S, U8) for z in range(PASSES)]
+        moves = [(z, i) for i in range(4) for z in range(PASSES)]
+        for z, i in moves:
+            queue = nc.gpsimd if (z, i) == moves[-1] else nc.sync
+            src = ROW0 + 16 * z + i
+            queue.dma_start(planes[z][4 * z + i : P : 32, :].bitcast(I32), picked_rows[src : src + 13 : 4, :].bitcast(I32))
 
         def x_scale(z, first, count):
-            if first < V:
-                return scale_early[z][4 * z :, first : first + count]
-            return scale_late[z][4 * z :, first - V : first - V + count]
+            return planes[z][4 * z :, first : first + count]
 
-        def multiply(first, moving):
+        quantized = [quantize(0, regroup(0, raws[0], placed_at("grouped0", PASSES * N * PACK, BF16, AT_RAW2)))]
+        raw2 = placed_at("raw2", PASSES * PACK * N, F32, AT_RAW2)
+        load_weight(nc.gpsimd, 2, raw2)
+
+        def multiply(first, moving, bank=None):
             codes, scale = quantized[first // V]
             count = moving[0].shape[1]
-            acc = psum.tile([P, count], F32, name=f"acc{first}")
+            acc = psum.tile([P, count], F32, name=f"acc{first}", tag=bank or f"acc{first}")
             spans = [(0, CHUNK), (CHUNK, count)] if count == V - CHUNK else [(0, count)]
             steps = [(z, span) for z in range(PASSES) for span in spans]
             for z, (lo, hi) in steps:
@@ -142,8 +128,8 @@ def tile_picked_spconv_none_p_kernel(tc, x_words, x_scales, w1, w2, w3, offs, to
                 )
             return acc
 
-        def leave(first, moving):
-            acc = multiply(first, moving)
+        def leave(first, moving, bank=None):
+            acc = multiply(first, moving, bank)
             y = sbuf(f"y{first}", acc.shape[1], F32)
             nc.scalar.copy(y[:], acc[:])
             return y
@@ -152,12 +138,15 @@ def tile_picked_spconv_none_p_kernel(tc, x_words, x_scales, w1, w2, w3, offs, to
             nc.scalar.activation(window(first // V, first % V, y.shape[1]), y[:], COPY)
 
         a_early = sbuf("a_early", EARLY, U32)
-        b_first = sbuf("b_first", CHUNK, U32, "after_first_product")
+        b_first = placed_at("b_first", CHUNK, U32, AT_FIRST)
         b_early = sbuf("b_early", 2 * V - CHUNK, U32)
+        b_late = placed_at("b_late", HALF, U32, AT_LATE)
         gather_words(0, 0, a_early[:])
+        quantized.append(quantize(1, regroup(1, raws[1], sbuf("grouped1", PASSES * N * PACK, BF16))))
         gather_words(1, 0, b_first[:])
         gather_words(1, CHUNK, b_early[:, 0 : V - CHUNK])
         gather_words(1, V, b_early[:, V - CHUNK :])
+        gather_words(1, 2 * V, b_late[:])
 
         def early(first, count):
             return a_early[:, first : first + count], b_early[:, first - CHUNK : first - CHUNK + count]
@@ -165,26 +154,22 @@ def tile_picked_spconv_none_p_kernel(tc, x_words, x_scales, w1, w2, w3, offs, to
         scatter_on_scalar(0, leave(0, (a_early[:, 0:CHUNK], b_first[:])))
         scatter_on_scalar(CHUNK, leave(CHUNK, early(CHUNK, V - CHUNK)))
 
-        a_mid = sbuf("a_mid", 2 * V - EARLY, U32, "after_first_product")
-        gather_words(0, EARLY, a_mid[:])
-        quantized.append(quantize(1, regroup(1, raw1, sbuf("grouped1", PASSES * N * PACK, BF16, "grouped_late"))))
-        y1_first = leave(V, early(V, CHUNK))
-        late = placed_at("late", 3 * HALF, U32, AT_RAW1)
-        a_late, b_late = late[:, 0:V], late[:, V:]
-        gather_words(0, 2 * V, a_late)
-        gather_words(1, 2 * V, b_late)
-        quantized.append(quantize(2, regroup(2, raw2, sbuf("grouped2", PASSES * N * PACK, BF16, "grouped_late"))))
-        y1_rest = placed_at("y1_rest", V - CHUNK, F32, AT_RAW2 + 1024)
-        nc.vector.tensor_copy(y1_rest[:], multiply(EARLY, (a_mid[:], b_early[:, EARLY - CHUNK :]))[:])
-        b_last = placed_at("b_last", HALF, U32, AT_RAW2)
-        gather_words(1, 2 * V + HALF, b_last[:])
-
-        y2_a = leave(2 * V, (a_late[:, 0:HALF], b_late))
-        scatter_on_scalar(V, y1_first)
-        nc.vector.tensor_copy(window(1, CHUNK, V - CHUNK), y1_rest[:])
-        y2_b = leave(2 * V + HALF, (a_late[:, HALF:], b_last[:]))
+        a_last = placed_at("a_last", HALF, U32, AT_FIRST - 768)
+        gather_words(0, EARLY, a_last[:])
+        grouped2 = regroup(2, raw2, placed_at("grouped2", PASSES * N * PACK, BF16, AT_FIRST + 256))
+        acc1 = multiply(V, early(V, V))
+        y1_a = placed_at("y1_a", HALF, F32, AT_RAW2)
+        nc.vector.tensor_copy(y1_a[:], acc1[:, 0:HALF])
+        quantized.append(quantize(2, grouped2))
+        nc.vector.tensor_copy(window(1, 0, HALF), y1_a[:])
+        y2_a = leave(2 * V, (a_early[:, 2 * V :], b_late[:]), "last")
+        b_last = placed_at("b_last", HALF, U32, AT_LATE + 512)
+        y1_b = placed_at("y1_b", HALF, F32, AT_LATE - 512)
+        nc.vector.tensor_copy(y1_b[:], acc1[:, HALF:])
+        gather_words(1, EARLY, b_last[:])
+        nc.vector.tensor_copy(window(1, HALF, HALF), y1_b[:])
         scatter_on_scalar(2 * V, y2_a)
-        scatter_on_scalar(2 * V + HALF, y2_b)
+        scatter_on_scalar(EARLY, leave(EARLY, (a_last[:], b_last[:]), "last"))
 
         pair = sbuf("pair", U, F32)
         for half in (slice(0, U // 2), slice(U // 2, U)):

@@ -81,10 +81,10 @@ def tile_picked_spconv_none_p_kernel(tc, x_words, x_scales, w1, w2, w3, offs, to
         nc.sync.dma_start(scale_table[ROW0:P, :].bitcast(I32), x_scales.rearrange("z q c -> (z q) c").bitcast(I32))
         nc.sync.dma_start(picks[:], offs)
         nc.vector.memset(scale_table[0:ROW0, :].bitcast(I32), 0)
-        for tile, dram in zip(maps, (to1, to2, to3)):
-            nc.sync.dma_start(tile[:], dram)
         load_weight(nc.sync, 0, raws[0])
         load_words(0)
+        for tile, dram in zip(maps, (to1, to2, to3)):
+            nc.sync.dma_start(tile[:], dram)
         load_weight(nc.sync, 1, raws[1])
         load_words(1)
 
@@ -165,7 +165,7 @@ def tile_picked_spconv_none_p_kernel(tc, x_words, x_scales, w1, w2, w3, offs, to
         y2_a = leave(2 * V, (a_early[:, 2 * V :], b_late[:]), "last")
         b_last = placed_at("b_last", HALF, U32, AT_LATE + 512)
         y1_b = placed_at("y1_b", HALF, F32, AT_LATE - 512)
-        nc.vector.tensor_copy(y1_b[:], acc1[:, HALF:])
+        nc.scalar.copy(y1_b[:], acc1[:, HALF:])
         gather_words(1, EARLY, b_last[:])
         nc.vector.tensor_copy(window(1, HALF, HALF), y1_b[:])
         scatter_on_scalar(2 * V, y2_a)

@@ -6,15 +6,18 @@ K, T, S, V, N, U = 1024, 2048, 1536, 512, 128, 1024
 TAPS = 3
 P = 128
 PACK = 4
+QUADS = 4
 PASSES = K // (P * PACK)
 HALF = V // 2
 CHUNK = 128
 ROW0 = P - 16 * PASSES
-EARLY = 2 * V + HALF
+EARLY = 2 * V
 STORE_COLS = 256
+BANK = 2048
 AT_RAW2 = 0
-AT_FIRST = 5120
-AT_LATE = 8192
+AT_GROUPED2 = 4096
+AT_FIRST = 6144
+AT_THIRD = 7168
 FLOPS = 2 * K * N * S
 
 F32 = mybir.dt.float32
@@ -37,11 +40,14 @@ def tile_picked_spconv_none_p_kernel(tc, x_words, x_scales, w1, w2, w3, offs, to
         reuse = ctx.enter_context(tc.tile_pool(name="reuse", bufs=1))
         psum = ctx.enter_context(tc.psum_pool(name="psum", bufs=1))
 
-        def sbuf(name, cols, dtype, tag=None):
-            return keep.tile([P, cols], dtype, name=name, tag=tag or name, align_bytes=64)
+        def sbuf(name, cols, dtype):
+            return keep.tile([P, cols], dtype, name=name, align_bytes=64)
 
         def placed_at(name, cols, dtype, offset):
             return reuse.tile([P, cols], dtype, name=name, align_bytes=64, offset=offset)
+
+        def bank_at(name, cols, bank):
+            return psum.tile([P, cols], F32, name=name, offset=bank * BANK)
 
         picks = keep.tile([P, S // 16], U16, name="picks")
         maps = [keep.tile([P, V // 16], U16, name=f"map{d}") for d in range(TAPS)]
@@ -52,8 +58,8 @@ def tile_picked_spconv_none_p_kernel(tc, x_words, x_scales, w1, w2, w3, offs, to
         def load_words(z):
             nc.sync.dma_start(word_tables[z][:], x_words[z].rearrange("p c r -> p (c r)").bitcast(I32))
 
-        def load_weight(queue, d, raw):
-            queue.dma_start(raw[:].rearrange("p (z r) -> p z r", z=PASSES), weights[d].rearrange("(z p j) m -> p z (j m)", z=PASSES, j=PACK))
+        def load_weight(d, raw):
+            nc.sync.dma_start(raw[:].rearrange("p (z r) -> p z r", z=PASSES), weights[d].rearrange("(z p j) m -> p z (j m)", z=PASSES, j=PACK))
 
         def regroup(d, raw, grouped):
             src = raw[:].rearrange("p (z j m) -> p z m j", z=PASSES, j=PACK)
@@ -78,14 +84,16 @@ def tile_picked_spconv_none_p_kernel(tc, x_words, x_scales, w1, w2, w3, offs, to
             return placed[d][:].indirect(maps[d][:, first // 16 : (first + count) // 16])
 
         raws = [sbuf(f"raw{d}", PASSES * PACK * N, F32) for d in range(2)]
-        nc.sync.dma_start(scale_table[ROW0:P, :].bitcast(I32), x_scales.rearrange("z q c -> (z q) c").bitcast(I32))
+        for z in range(PASSES):
+            rows = scale_table[ROW0 + 16 * z : ROW0 + 16 * (z + 1), :]
+            nc.sync.dma_start(rows.bitcast(I32), x_scales[z].bitcast(I32).rearrange("(q i) c -> i q c", q=QUADS))
         nc.sync.dma_start(picks[:], offs)
         nc.vector.memset(scale_table[0:ROW0, :].bitcast(I32), 0)
-        load_weight(nc.sync, 0, raws[0])
+        load_weight(0, raws[0])
         load_words(0)
         for tile, dram in zip(maps, (to1, to2, to3)):
             nc.sync.dma_start(tile[:], dram)
-        load_weight(nc.sync, 1, raws[1])
+        load_weight(1, raws[1])
         load_words(1)
 
         zero = sbuf("zero", 1, F32)
@@ -96,80 +104,91 @@ def tile_picked_spconv_none_p_kernel(tc, x_words, x_scales, w1, w2, w3, offs, to
 
         picked_rows = sbuf("picked_rows", S, U8)
         nc.vector.tensor_copy(picked_rows[:], scale_table[:].indirect(picks[:]))
-        planes = [sbuf(f"plane{z}", S, U8) for z in range(PASSES)]
-        moves = [(z, i) for i in range(4) for z in range(PASSES)]
-        for z, i in moves:
-            queue = nc.gpsimd if (z, i) == moves[-1] else nc.sync
-            src = ROW0 + 16 * z + i
-            queue.dma_start(planes[z][4 * z + i : P : 32, :].bitcast(I32), picked_rows[src : src + 13 : 4, :].bitcast(I32))
-
-        def x_scale(z, first, count):
-            return planes[z][4 * z :, first : first + count]
+        planes = sbuf("planes", S, U8)
+        for q in range(QUADS):
+            nc.sync.dma_start(planes[32 * q : 32 * q + 8, :].bitcast(I32), picked_rows[ROW0 + q : P : QUADS, :].bitcast(I32))
 
         quantized = [quantize(0, regroup(0, raws[0], placed_at("grouped0", PASSES * N * PACK, BF16, AT_RAW2)))]
         raw2 = placed_at("raw2", PASSES * PACK * N, F32, AT_RAW2)
-        load_weight(nc.gpsimd, 2, raw2)
+        load_weight(2, raw2)
 
-        def multiply(first, moving, bank=None):
-            codes, scale = quantized[first // V]
-            count = moving[0].shape[1]
-            acc = psum.tile([P, count], F32, name=f"acc{first}", tag=bank or f"acc{first}")
-            spans = [(0, CHUNK), (CHUNK, count)] if count == V - CHUNK else [(0, count)]
+        def multiply(acc, spans):
             steps = [(z, span) for z in range(PASSES) for span in spans]
-            for z, (lo, hi) in steps:
+            for z, (at, first, moving) in steps:
+                codes, scale = quantized[first // V]
+                count = moving[0].shape[1]
                 nc.tensor.matmul_mx(
-                    out=acc[:, lo:hi],
+                    out=acc[:, at : at + count],
                     lhsT=codes[:, z * N : (z + 1) * N].bitcast(FP8X4),
                     lhsT_scale=scale[:, z * N : (z + 1) * N],
-                    rhs=moving[z][:, lo:hi].bitcast(FP8X4),
-                    rhs_scale=x_scale(z, first + lo, hi - lo),
-                    start=((z, (lo, hi)) == steps[0]),
-                    stop=((z, (lo, hi)) == steps[-1]),
+                    rhs=moving[z].bitcast(FP8X4),
+                    rhs_scale=planes[4 * z :, first : first + count],
+                    start=((z, at) == (0, spans[0][0])),
+                    stop=((z, at) == (PASSES - 1, spans[-1][0])),
                 )
-            return acc
-
-        def leave(first, moving, bank=None):
-            acc = multiply(first, moving, bank)
-            y = sbuf(f"y{first}", acc.shape[1], F32)
-            nc.scalar.copy(y[:], acc[:])
-            return y
 
         def scatter_on_scalar(first, y):
-            nc.scalar.activation(window(first // V, first % V, y.shape[1]), y[:], COPY)
+            nc.scalar.activation(window(first // V, first % V, y.shape[1]), y, COPY)
+
+        def scatter_on_vector(first, y):
+            nc.vector.tensor_copy(window(first // V, first % V, y.shape[1]), y)
 
         a_early = sbuf("a_early", EARLY, U32)
         b_first = placed_at("b_first", CHUNK, U32, AT_FIRST)
-        b_early = sbuf("b_early", 2 * V - CHUNK, U32)
-        b_late = placed_at("b_late", HALF, U32, AT_LATE)
+        b_early = sbuf("b_early", EARLY - CHUNK, U32)
+        b_third = placed_at("b_third", HALF, U32, AT_THIRD)
         gather_words(0, 0, a_early[:])
         quantized.append(quantize(1, regroup(1, raws[1], sbuf("grouped1", PASSES * N * PACK, BF16))))
         gather_words(1, 0, b_first[:])
         gather_words(1, CHUNK, b_early[:, 0 : V - CHUNK])
-        gather_words(1, V, b_early[:, V - CHUNK :])
-        gather_words(1, 2 * V, b_late[:])
+        gather_words(1, V, b_early[:, V - CHUNK : V - CHUNK + HALF])
+        gather_words(1, V + HALF, b_early[:, V - CHUNK + HALF :])
+        gather_words(1, 2 * V, b_third[:])
 
         def early(first, count):
             return a_early[:, first : first + count], b_early[:, first - CHUNK : first - CHUNK + count]
 
-        scatter_on_scalar(0, leave(0, (a_early[:, 0:CHUNK], b_first[:])))
-        scatter_on_scalar(CHUNK, leave(CHUNK, early(CHUNK, V - CHUNK)))
+        acc_first = bank_at("acc_first", CHUNK, 0)
+        multiply(acc_first, [(0, 0, (a_early[:, 0:CHUNK], b_first[:]))])
+        y0 = sbuf("y0", V, F32)
+        nc.scalar.copy(y0[:, 0:CHUNK], acc_first[:, 0:CHUNK])
+        scatter_on_scalar(0, y0[:, 0:CHUNK])
 
-        a_last = placed_at("a_last", HALF, U32, AT_FIRST - 768)
-        gather_words(0, EARLY, a_last[:])
-        grouped2 = regroup(2, raw2, placed_at("grouped2", PASSES * N * PACK, BF16, AT_FIRST + 256))
-        acc1 = multiply(V, early(V, V))
-        y1_a = placed_at("y1_a", HALF, F32, AT_RAW2)
-        nc.vector.tensor_copy(y1_a[:], acc1[:, 0:HALF])
+        a_third = placed_at("a_third", HALF, U32, AT_FIRST)
+        gather_words(0, 2 * V, a_third[:])
+
+        acc0 = bank_at("acc0", V - CHUNK, 1)
+        multiply(acc0, [(0, CHUNK, early(CHUNK, CHUNK)), (CHUNK, HALF, early(HALF, HALF))])
+        acc1 = bank_at("acc1", HALF, 0)
+        multiply(acc1, [(0, V, early(V, HALF))])
+        y1 = sbuf("y1", V - CHUNK, F32)
+        nc.scalar.copy(y0[:, CHUNK:], acc0[:])
+        nc.scalar.copy(y1[:, 0:CHUNK], acc1[:, CHUNK:])
+        scatter_on_scalar(CHUNK, y0[:, CHUNK:])
+
+        grouped2 = regroup(2, raw2, placed_at("grouped2", PASSES * N * PACK, BF16, AT_GROUPED2))
+        y1_first = placed_at("y1_first", CHUNK, F32, AT_RAW2)
+        nc.vector.tensor_copy(y1_first[:], acc1[:, 0:CHUNK])
         quantized.append(quantize(2, grouped2))
-        nc.vector.tensor_copy(window(1, 0, HALF), y1_a[:])
-        y2_a = leave(2 * V, (a_early[:, 2 * V :], b_late[:]), "last")
-        b_last = placed_at("b_last", HALF, U32, AT_LATE + 512)
-        y1_b = placed_at("y1_b", HALF, F32, AT_LATE - 512)
-        nc.scalar.copy(y1_b[:], acc1[:, HALF:])
-        gather_words(1, EARLY, b_last[:])
-        nc.vector.tensor_copy(window(1, HALF, HALF), y1_b[:])
-        scatter_on_scalar(2 * V, y2_a)
-        scatter_on_scalar(EARLY, leave(EARLY, (a_last[:], b_last[:]), "last"))
+        scatter_on_vector(V, y1_first[:])
+        a_last = placed_at("a_last", HALF, U32, AT_GROUPED2)
+        gather_words(0, 2 * V + HALF, a_last[:])
+        scatter_on_vector(V + CHUNK, y1[:, 0:CHUNK])
+
+        acc2 = bank_at("acc2", V, 2)
+        multiply(acc2, [(HALF, V + HALF, early(V + HALF, HALF))])
+        multiply(acc2, [(0, 2 * V, (a_third[:], b_third[:]))])
+        b_last = placed_at("b_last", HALF, U32, AT_THIRD)
+        gather_words(1, 2 * V + HALF, b_last[:])
+        y2 = sbuf("y2", V, F32)
+        nc.scalar.copy(y2[:, 0:HALF], acc2[:, 0:HALF])
+        nc.scalar.copy(y1[:, CHUNK:], acc2[:, HALF:])
+        scatter_on_scalar(2 * V, y2[:, 0:HALF])
+        scatter_on_vector(V + HALF, y1[:, CHUNK:])
+        acc_last = bank_at("acc_last", HALF, 2)
+        multiply(acc_last, [(0, 2 * V + HALF, (a_last[:], b_last[:]))])
+        nc.scalar.copy(y2[:, HALF:], acc_last[:])
+        scatter_on_scalar(2 * V + HALF, y2[:, HALF:])
 
         pair = sbuf("pair", U, F32)
         for half in (slice(0, U // 2), slice(U // 2, U)):

@@ -11,13 +11,18 @@ PASSES = K // (P * PACK)
 HALF = V // 2
 CHUNK = 128
 ROW0 = P - 16 * PASSES
-EARLY = 2 * V
+EARLY = 2 * V + CHUNK
 STORE_COLS = 256
 BANK = 2048
 AT_RAW2 = 0
-AT_GROUPED2 = 4096
-AT_FIRST = 6144
-AT_THIRD = 7168
+AT_GROUPED0 = 3072
+AT_LATE_PLANES = 4096
+AT_GROUPED2 = 6144
+AT_FIRST = 8192
+AT_THIRD = 9216
+AT_SECOND = 10240
+AT_TAP1 = 12288
+AT_WORDS1 = 14336
 FLOPS = 2 * K * N * S
 
 F32 = mybir.dt.float32
@@ -52,7 +57,8 @@ def tile_picked_spconv_none_p_kernel(tc, x_words, x_scales, w1, w2, w3, offs, to
         picks = keep.tile([P, S // 16], U16, name="picks")
         maps = [keep.tile([P, V // 16], U16, name=f"map{d}") for d in range(TAPS)]
         scale_table = sbuf("scale_table", T, U8)
-        word_tables = [sbuf(f"word_table{z}", T, I32) for z in range(PASSES)]
+        zero = placed_at("zero", 1, F32, AT_WORDS1)
+        word_tables = [sbuf("word_table0", T, I32), placed_at("word_table1", T, I32, AT_WORDS1)]
         placed = [sbuf(f"placed{d}", U, F32) for d in range(TAPS)]
 
         def load_words(z):
@@ -70,8 +76,8 @@ def tile_picked_spconv_none_p_kernel(tc, x_words, x_scales, w1, w2, w3, offs, to
                 nc.gpsimd.tensor_scalar(dst, src, 1.0, 0.0, MULT, ADD)
             return grouped
 
-        def quantize(d, grouped):
-            codes = sbuf(f"w_codes{d}", PASSES * N, U32)
+        def quantize(d, grouped, at=None):
+            codes = sbuf(f"w_codes{d}", PASSES * N, U32) if at is None else placed_at(f"w_codes{d}", PASSES * N, U32, at)
             scale = sbuf(f"w_scale{d}", PASSES * N, U8)
             nc.vector.quantize_mx(out=codes[:].bitcast(FP8X4), scales=scale[:], in_=grouped[:])
             return codes, scale
@@ -84,33 +90,46 @@ def tile_picked_spconv_none_p_kernel(tc, x_words, x_scales, w1, w2, w3, offs, to
             return placed[d][:].indirect(maps[d][:, first // 16 : (first + count) // 16])
 
         raws = [sbuf(f"raw{d}", PASSES * PACK * N, F32) for d in range(2)]
-        for z in range(PASSES):
-            rows = scale_table[ROW0 + 16 * z : ROW0 + 16 * (z + 1), :]
-            nc.sync.dma_start(rows.bitcast(I32), x_scales[z].bitcast(I32).rearrange("(q i) c -> i q c", q=QUADS))
+        nc.sync.dma_start(scale_table[ROW0:P, :].bitcast(I32), x_scales.bitcast(I32).rearrange("z r c -> r z c"))
         nc.sync.dma_start(picks[:], offs)
         nc.vector.memset(scale_table[0:ROW0, :].bitcast(I32), 0)
         load_weight(0, raws[0])
-        load_words(0)
         for tile, dram in zip(maps, (to1, to2, to3)):
             nc.sync.dma_start(tile[:], dram)
+        load_words(0)
         load_weight(1, raws[1])
-        load_words(1)
 
-        zero = sbuf("zero", 1, F32)
         nc.vector.memset(zero[:], 0.0)
         nc.vector.memset(placed[1][:], 0.0)
         for d in (0, 2):
             nc.scalar.activation(placed[d][:], zero[:].to_broadcast([P, U]), COPY)
 
-        picked_rows = sbuf("picked_rows", S, U8)
-        nc.vector.tensor_copy(picked_rows[:], scale_table[:].indirect(picks[:]))
-        planes = sbuf("planes", S, U8)
-        for q in range(QUADS):
-            nc.sync.dma_start(planes[32 * q : 32 * q + 8, :].bitcast(I32), picked_rows[ROW0 + q : P : QUADS, :].bitcast(I32))
+        def gather_scales(name, first, count):
+            picked = sbuf(name, count, U8)
+            nc.vector.tensor_copy(picked[:], scale_table[:].indirect(picks[:, first // 16 : (first + count) // 16]))
+            return picked
 
-        quantized = [quantize(0, regroup(0, raws[0], placed_at("grouped0", PASSES * N * PACK, BF16, AT_RAW2)))]
+        def move_rows(picked, planes):
+            for q in range(QUADS):
+                rows = planes[32 * q : 32 * q + 4, :].bitcast(I32).rearrange("p (z c) -> p z c", z=PASSES)
+                nc.sync.dma_start(rows, picked[ROW0 + 8 * q : ROW0 + 8 * (q + 1), :].bitcast(I32))
+
+        first_planes = sbuf("first_planes", PASSES * V, U8)
+        move_rows(gather_scales("first_rows", 0, V), first_planes)
+        load_words(1)
+        late_rows = gather_scales("late_rows", V, S - V)
+
+        quantized = [quantize(0, regroup(0, raws[0], placed_at("grouped0", PASSES * N * PACK, BF16, AT_GROUPED0)))]
         raw2 = placed_at("raw2", PASSES * PACK * N, F32, AT_RAW2)
         load_weight(2, raw2)
+        late_planes = placed_at("late_planes", PASSES * (S - V), U8, AT_LATE_PLANES)
+        move_rows(late_rows, late_planes)
+
+        def x_scale(z, first, count):
+            if first < V:
+                return first_planes[:, z * V + first : z * V + first + count]
+            at = z * (S - V) + first - V
+            return late_planes[:, at : at + count]
 
         def multiply(acc, spans):
             steps = [(z, span) for z in range(PASSES) for span in spans]
@@ -122,7 +141,7 @@ def tile_picked_spconv_none_p_kernel(tc, x_words, x_scales, w1, w2, w3, offs, to
                     lhsT=codes[:, z * N : (z + 1) * N].bitcast(FP8X4),
                     lhsT_scale=scale[:, z * N : (z + 1) * N],
                     rhs=moving[z].bitcast(FP8X4),
-                    rhs_scale=planes[4 * z :, first : first + count],
+                    rhs_scale=x_scale(z, first, count),
                     start=((z, at) == (0, spans[0][0])),
                     stop=((z, at) == (PASSES - 1, spans[-1][0])),
                 )
@@ -135,56 +154,60 @@ def tile_picked_spconv_none_p_kernel(tc, x_words, x_scales, w1, w2, w3, offs, to
 
         a_early = sbuf("a_early", EARLY, U32)
         b_first = placed_at("b_first", CHUNK, U32, AT_FIRST)
-        b_early = sbuf("b_early", EARLY - CHUNK, U32)
+        b_second = placed_at("b_second", V - CHUNK, U32, AT_SECOND)
+        b_tap1 = placed_at("b_tap1", V, U32, AT_TAP1)
         b_third = placed_at("b_third", HALF, U32, AT_THIRD)
         gather_words(0, 0, a_early[:])
         quantized.append(quantize(1, regroup(1, raws[1], sbuf("grouped1", PASSES * N * PACK, BF16))))
         gather_words(1, 0, b_first[:])
-        gather_words(1, CHUNK, b_early[:, 0 : V - CHUNK])
-        gather_words(1, V, b_early[:, V - CHUNK : V - CHUNK + HALF])
-        gather_words(1, V + HALF, b_early[:, V - CHUNK + HALF :])
+        gather_words(1, CHUNK, b_second[:])
+        gather_words(1, V, b_tap1[:])
         gather_words(1, 2 * V, b_third[:])
 
         def early(first, count):
-            return a_early[:, first : first + count], b_early[:, first - CHUNK : first - CHUNK + count]
+            pass1 = b_second[:, first - CHUNK : first - CHUNK + count] if first < V else b_tap1[:, first - V : first - V + count]
+            return a_early[:, first : first + count], pass1
 
         acc_first = bank_at("acc_first", CHUNK, 0)
         multiply(acc_first, [(0, 0, (a_early[:, 0:CHUNK], b_first[:]))])
-        y0 = sbuf("y0", V, F32)
-        nc.scalar.copy(y0[:, 0:CHUNK], acc_first[:, 0:CHUNK])
-        scatter_on_scalar(0, y0[:, 0:CHUNK])
+        y_first = sbuf("y_first", CHUNK, F32)
+        nc.scalar.copy(y_first[:], acc_first[:])
+        scatter_on_scalar(0, y_first[:])
 
-        a_third = placed_at("a_third", HALF, U32, AT_FIRST)
-        gather_words(0, 2 * V, a_third[:])
+        a_third = placed_at("a_third", CHUNK, U32, AT_FIRST)
+        gather_words(0, EARLY, a_third[:])
 
-        acc0 = bank_at("acc0", V - CHUNK, 1)
-        multiply(acc0, [(0, CHUNK, early(CHUNK, CHUNK)), (CHUNK, HALF, early(HALF, HALF))])
-        acc1 = bank_at("acc1", HALF, 0)
+        acc0 = bank_at("acc0", HALF, 1)
+        multiply(acc0, [(0, HALF, early(HALF, HALF))])
+        acc_second = bank_at("acc_second", CHUNK, 0)
+        multiply(acc_second, [(0, CHUNK, early(CHUNK, CHUNK))])
+        acc1 = bank_at("acc1", HALF, 3)
         multiply(acc1, [(0, V, early(V, HALF))])
-        y1 = sbuf("y1", V - CHUNK, F32)
+        y0 = placed_at("y0", V - CHUNK, F32, AT_SECOND)
         nc.scalar.copy(y0[:, CHUNK:], acc0[:])
-        nc.scalar.copy(y1[:, 0:CHUNK], acc1[:, CHUNK:])
-        scatter_on_scalar(CHUNK, y0[:, CHUNK:])
-
-        grouped2 = regroup(2, raw2, placed_at("grouped2", PASSES * N * PACK, BF16, AT_GROUPED2))
-        y1_first = placed_at("y1_first", CHUNK, F32, AT_RAW2)
-        nc.vector.tensor_copy(y1_first[:], acc1[:, 0:CHUNK])
-        quantized.append(quantize(2, grouped2))
-        scatter_on_vector(V, y1_first[:])
-        a_last = placed_at("a_last", HALF, U32, AT_GROUPED2)
-        gather_words(0, 2 * V + HALF, a_last[:])
-        scatter_on_vector(V + CHUNK, y1[:, 0:CHUNK])
+        nc.scalar.copy(y0[:, 0:CHUNK], acc_second[:])
+        scatter_on_scalar(CHUNK, y0[:])
 
         acc2 = bank_at("acc2", V, 2)
         multiply(acc2, [(HALF, V + HALF, early(V + HALF, HALF))])
-        multiply(acc2, [(0, 2 * V, (a_third[:], b_third[:]))])
+        grouped2 = regroup(2, raw2, placed_at("grouped2", PASSES * N * PACK, BF16, AT_GROUPED2))
+        y1_first = placed_at("y1_first", HALF, F32, AT_RAW2)
+        nc.vector.tensor_copy(y1_first[:], acc1[:])
+        quantized.append(quantize(2, grouped2, AT_TAP1))
+        scatter_on_vector(V, y1_first[:, 0:CHUNK])
+        a_last = placed_at("a_last", HALF, U32, AT_GROUPED2)
+        gather_words(0, 2 * V + HALF, a_last[:])
+        scatter_on_vector(V + CHUNK, y1_first[:, CHUNK:])
+
+        multiply(acc2, [(0, 2 * V, (a_early[:, 2 * V :], b_third[:, 0:CHUNK])), (CHUNK, EARLY, (a_third[:], b_third[:, CHUNK:]))])
         b_last = placed_at("b_last", HALF, U32, AT_THIRD)
         gather_words(1, 2 * V + HALF, b_last[:])
         y2 = sbuf("y2", V, F32)
         nc.scalar.copy(y2[:, 0:HALF], acc2[:, 0:HALF])
-        nc.scalar.copy(y1[:, CHUNK:], acc2[:, HALF:])
+        y1_last = sbuf("y1_last", HALF, F32)
+        nc.scalar.copy(y1_last[:], acc2[:, HALF:])
         scatter_on_scalar(2 * V, y2[:, 0:HALF])
-        scatter_on_vector(V + HALF, y1[:, CHUNK:])
+        scatter_on_vector(V + HALF, y1_last[:])
         acc_last = bank_at("acc_last", HALF, 2)
         multiply(acc_last, [(0, 2 * V + HALF, (a_last[:], b_last[:]))])
         nc.scalar.copy(y2[:, HALF:], acc_last[:])

@@ -14,15 +14,16 @@ ROW0 = P - 16 * PASSES
 EARLY = 2 * V + CHUNK
 STORE_COLS = 256
 BANK = 2048
-AT_RAW2 = 0
-AT_GROUPED0 = 3072
+AT_RAW2 = 1024
+AT_GROUPED0 = 2560
 AT_LATE_PLANES = 4096
 AT_GROUPED2 = 6144
 AT_FIRST = 8192
 AT_THIRD = 9216
 AT_SECOND = 10240
 AT_TAP1 = 12288
-AT_WORDS1 = 14336
+AT_RAW0 = 14336
+AT_WORDS1 = 18432
 FLOPS = 2 * K * N * S
 
 F32 = mybir.dt.float32
@@ -70,11 +71,15 @@ def tile_picked_spconv_none_p_kernel(tc, x_words, x_scales, w1, w2, w3, offs, to
         def regroup(d, raw, grouped):
             src = raw[:].rearrange("p (z j m) -> p z m j", z=PASSES, j=PACK)
             dst = grouped[:].rearrange("p (z m j) -> p z m j", z=PASSES, j=PACK)
-            if d < 2:
-                nc.scalar.copy(dst, src)
-            else:
-                nc.gpsimd.tensor_scalar(dst, src, 1.0, 0.0, MULT, ADD)
+            nc.scalar.copy(dst, src)
             return grouped
+
+        def load_last_weight(z, raw):
+            nc.sync.dma_start(raw[:], w3[z * P * PACK : (z + 1) * P * PACK, :].rearrange("(p j) m -> p (j m)", j=PACK))
+
+        def regroup_last_weight(z, raw, grouped):
+            dst = grouped[:, z * N * PACK : (z + 1) * N * PACK].rearrange("p (m j) -> p m j", j=PACK)
+            nc.gpsimd.tensor_scalar(dst, raw[:].rearrange("p (j m) -> p m j", j=PACK), 1.0, 0.0, MULT, ADD)
 
         def quantize(d, grouped, at=None):
             codes = sbuf(f"w_codes{d}", PASSES * N, U32) if at is None else placed_at(f"w_codes{d}", PASSES * N, U32, at)
@@ -89,7 +94,7 @@ def tile_picked_spconv_none_p_kernel(tc, x_words, x_scales, w1, w2, w3, offs, to
         def window(d, first, count):
             return placed[d][:].indirect(maps[d][:, first // 16 : (first + count) // 16])
 
-        raws = [sbuf(f"raw{d}", PASSES * PACK * N, F32) for d in range(2)]
+        raws = [placed_at("raw0", PASSES * PACK * N, F32, AT_RAW0), sbuf("raw1", PASSES * PACK * N, F32)]
         nc.sync.dma_start(scale_table[ROW0:P, :].bitcast(I32), x_scales.bitcast(I32).rearrange("z r c -> r z c"))
         nc.sync.dma_start(picks[:], offs)
         nc.vector.memset(scale_table[0:ROW0, :].bitcast(I32), 0)
@@ -120,10 +125,11 @@ def tile_picked_spconv_none_p_kernel(tc, x_words, x_scales, w1, w2, w3, offs, to
         late_rows = gather_scales("late_rows", V, S - V)
 
         quantized = [quantize(0, regroup(0, raws[0], placed_at("grouped0", PASSES * N * PACK, BF16, AT_GROUPED0)))]
-        raw2 = placed_at("raw2", PASSES * PACK * N, F32, AT_RAW2)
-        load_weight(2, raw2)
+        raw2 = [placed_at(f"raw2_{z}", PACK * N, F32, at) for z, at in enumerate((AT_RAW0, AT_RAW2))]
+        load_last_weight(0, raw2[0])
         late_planes = placed_at("late_planes", PASSES * (S - V), U8, AT_LATE_PLANES)
         move_rows(late_rows, late_planes)
+        load_last_weight(1, raw2[1])
 
         def x_scale(z, first, count):
             if first < V:
@@ -168,20 +174,20 @@ def tile_picked_spconv_none_p_kernel(tc, x_words, x_scales, w1, w2, w3, offs, to
             pass1 = b_second[:, first - CHUNK : first - CHUNK + count] if first < V else b_tap1[:, first - V : first - V + count]
             return a_early[:, first : first + count], pass1
 
-        acc_first = bank_at("acc_first", CHUNK, 0)
+        acc_first = bank_at("acc_first", 3 * V, 0)
         multiply(acc_first, [(0, 0, (a_early[:, 0:CHUNK], b_first[:]))])
         y_first = sbuf("y_first", CHUNK, F32)
-        nc.scalar.copy(y_first[:], acc_first[:])
+        nc.scalar.copy(y_first[:], acc_first[:, 0:CHUNK])
         scatter_on_scalar(0, y_first[:])
 
         a_third = placed_at("a_third", CHUNK, U32, AT_FIRST)
         gather_words(0, EARLY, a_third[:])
 
-        acc0 = bank_at("acc0", HALF, 1)
+        acc0 = bank_at("acc0", HALF, 3)
         multiply(acc0, [(0, HALF, early(HALF, HALF))])
         acc_second = bank_at("acc_second", CHUNK, 0)
         multiply(acc_second, [(0, CHUNK, early(CHUNK, CHUNK))])
-        acc1 = bank_at("acc1", HALF, 3)
+        acc1 = bank_at("acc1", HALF, 1)
         multiply(acc1, [(0, V, early(V, HALF))])
         y0 = placed_at("y0", V - CHUNK, F32, AT_SECOND)
         nc.scalar.copy(y0[:, CHUNK:], acc0[:])
@@ -190,7 +196,9 @@ def tile_picked_spconv_none_p_kernel(tc, x_words, x_scales, w1, w2, w3, offs, to
 
         acc2 = bank_at("acc2", V, 2)
         multiply(acc2, [(HALF, V + HALF, early(V + HALF, HALF))])
-        grouped2 = regroup(2, raw2, placed_at("grouped2", PASSES * N * PACK, BF16, AT_GROUPED2))
+        grouped2 = placed_at("grouped2", PASSES * N * PACK, BF16, AT_GROUPED2)
+        for z in range(PASSES):
+            regroup_last_weight(z, raw2[z], grouped2)
         y1_first = placed_at("y1_first", HALF, F32, AT_RAW2)
         nc.vector.tensor_copy(y1_first[:], acc1[:])
         quantized.append(quantize(2, grouped2, AT_TAP1))

@@ -11,18 +11,20 @@ PASSES = K // (P * PACK)
 HALF = V // 2
 CHUNK = 128
 ROW0 = P - 16 * PASSES
-EARLY = 2 * V + CHUNK
+EARLY = 2 * V
 STORE_COLS = 256
 BANK = 2048
 AT_RAW2 = 1024
 AT_GROUPED0 = 2560
 AT_LATE_PLANES = 4096
 AT_GROUPED2 = 6144
-AT_FIRST = 8192
-AT_THIRD = 9216
-AT_SECOND = 10240
-AT_TAP1 = 12288
-AT_RAW0 = 14336
+AT_SECOND = 8192
+AT_RAW0 = 12288
+AT_TAP1 = AT_RAW0 - 1984
+AT_TAP2 = AT_RAW0 + 64
+AT_FIRST = 0
+AT_THIRD = AT_RAW0 + 1088
+AT_RAW2_FIRST = AT_RAW0 + 2560
 AT_WORDS1 = 18432
 FLOPS = 2 * K * N * S
 
@@ -74,18 +76,23 @@ def tile_picked_spconv_none_p_kernel(tc, x_words, x_scales, w1, w2, w3, offs, to
             nc.scalar.copy(dst, src)
             return grouped
 
-        def load_last_weight(z, raw):
-            nc.sync.dma_start(raw[:], w3[z * P * PACK : (z + 1) * P * PACK, :].rearrange("(p j) m -> p (j m)", j=PACK))
+        def load_pass(d, z, raw):
+            nc.sync.dma_start(raw[:], weights[d][z * P * PACK : (z + 1) * P * PACK, :].rearrange("(p j) m -> p (j m)", j=PACK))
 
-        def regroup_last_weight(z, raw, grouped):
-            dst = grouped[:, z * N * PACK : (z + 1) * N * PACK].rearrange("p (m j) -> p m j", j=PACK)
-            nc.gpsimd.tensor_scalar(dst, raw[:].rearrange("p (j m) -> p m j", j=PACK), 1.0, 0.0, MULT, ADD)
+        def regroup_columns(engine, raw, grouped, lo, hi):
+            src = raw[:].rearrange("p (j m) -> p m j", j=PACK)[:, lo:hi, :]
+            dst = grouped.rearrange("p (m j) -> p m j", j=PACK)[:, lo:hi, :]
+            if engine is nc.scalar:
+                nc.scalar.copy(dst, src)
+            else:
+                nc.gpsimd.tensor_scalar(dst, src, 1.0, 0.0, MULT, ADD)
 
-        def quantize(d, grouped, at=None):
-            codes = sbuf(f"w_codes{d}", PASSES * N, U32) if at is None else placed_at(f"w_codes{d}", PASSES * N, U32, at)
-            scale = sbuf(f"w_scale{d}", PASSES * N, U8)
+        def quantize(name, grouped, at=None):
+            cols = grouped.shape[1] // PACK
+            codes = sbuf(f"codes_{name}", cols, U32) if at is None else placed_at(f"codes_{name}", cols, U32, at)
+            scale = sbuf(f"scale_{name}", cols, U8)
             nc.vector.quantize_mx(out=codes[:].bitcast(FP8X4), scales=scale[:], in_=grouped[:])
-            return codes, scale
+            return [(codes[:, c : c + N], scale[:, c : c + N]) for c in range(0, cols, N)]
 
         def gather_words(z, first, piece):
             count = piece.shape[1]
@@ -94,15 +101,16 @@ def tile_picked_spconv_none_p_kernel(tc, x_words, x_scales, w1, w2, w3, offs, to
         def window(d, first, count):
             return placed[d][:].indirect(maps[d][:, first // 16 : (first + count) // 16])
 
-        raws = [placed_at("raw0", PASSES * PACK * N, F32, AT_RAW0), sbuf("raw1", PASSES * PACK * N, F32)]
+        raw0 = placed_at("raw0", PASSES * PACK * N, F32, AT_RAW0)
+        raw1_first = sbuf("raw1_first", PACK * N, F32)
         nc.sync.dma_start(scale_table[ROW0:P, :].bitcast(I32), x_scales.bitcast(I32).rearrange("z r c -> r z c"))
         nc.sync.dma_start(picks[:], offs)
         nc.vector.memset(scale_table[0:ROW0, :].bitcast(I32), 0)
-        load_weight(0, raws[0])
+        load_weight(0, raw0)
         for tile, dram in zip(maps, (to1, to2, to3)):
             nc.sync.dma_start(tile[:], dram)
         load_words(0)
-        load_weight(1, raws[1])
+        load_pass(1, 0, raw1_first)
 
         nc.vector.memset(zero[:], 0.0)
         nc.vector.memset(placed[1][:], 0.0)
@@ -124,12 +132,14 @@ def tile_picked_spconv_none_p_kernel(tc, x_words, x_scales, w1, w2, w3, offs, to
         load_words(1)
         late_rows = gather_scales("late_rows", V, S - V)
 
-        quantized = [quantize(0, regroup(0, raws[0], placed_at("grouped0", PASSES * N * PACK, BF16, AT_GROUPED0)))]
-        raw2 = [placed_at(f"raw2_{z}", PACK * N, F32, at) for z, at in enumerate((AT_RAW0, AT_RAW2))]
-        load_last_weight(0, raw2[0])
+        quantized = [quantize("w1", regroup(0, raw0, placed_at("grouped0", PASSES * N * PACK, BF16, AT_GROUPED0)))]
+        raw1_last = placed_at("raw1_last", PACK * N, F32, AT_RAW0)
+        load_pass(1, 1, raw1_last)
+        raw2 = [placed_at(f"raw2_{z}", PACK * N, F32, at) for z, at in enumerate((AT_RAW2_FIRST, AT_RAW2))]
+        load_pass(2, 0, raw2[0])
         late_planes = placed_at("late_planes", PASSES * (S - V), U8, AT_LATE_PLANES)
         move_rows(late_rows, late_planes)
-        load_last_weight(1, raw2[1])
+        load_pass(2, 1, raw2[1])
 
         def x_scale(z, first, count):
             if first < V:
@@ -137,15 +147,15 @@ def tile_picked_spconv_none_p_kernel(tc, x_words, x_scales, w1, w2, w3, offs, to
             at = z * (S - V) + first - V
             return late_planes[:, at : at + count]
 
-        def multiply(acc, spans):
-            steps = [(z, span) for z in range(PASSES) for span in spans]
+        def multiply(acc, spans, passes=range(PASSES)):
+            steps = [(z, span) for z in passes for span in spans]
             for z, (at, first, moving) in steps:
-                codes, scale = quantized[first // V]
+                codes, scale = quantized[first // V][z]
                 count = moving[0].shape[1]
                 nc.tensor.matmul_mx(
                     out=acc[:, at : at + count],
-                    lhsT=codes[:, z * N : (z + 1) * N].bitcast(FP8X4),
-                    lhsT_scale=scale[:, z * N : (z + 1) * N],
+                    lhsT=codes.bitcast(FP8X4),
+                    lhsT_scale=scale,
                     rhs=moving[z].bitcast(FP8X4),
                     rhs_scale=x_scale(z, first, count),
                     start=((z, at) == (0, spans[0][0])),
@@ -161,14 +171,22 @@ def tile_picked_spconv_none_p_kernel(tc, x_words, x_scales, w1, w2, w3, offs, to
         a_early = sbuf("a_early", EARLY, U32)
         b_first = placed_at("b_first", CHUNK, U32, AT_FIRST)
         b_second = placed_at("b_second", V - CHUNK, U32, AT_SECOND)
-        b_tap1 = placed_at("b_tap1", V, U32, AT_TAP1)
-        b_third = placed_at("b_third", HALF, U32, AT_THIRD)
         gather_words(0, 0, a_early[:])
-        quantized.append(quantize(1, regroup(1, raws[1], sbuf("grouped1", PASSES * N * PACK, BF16))))
+        grouped1_first = sbuf("grouped1_first", N * PACK, BF16)
+        regroup_columns(nc.scalar, raw1_first, grouped1_first[:], 0, N)
+        w2_first = quantize("w2_first", grouped1_first)
         gather_words(1, 0, b_first[:])
         gather_words(1, CHUNK, b_second[:])
+        grouped1_last = placed_at("grouped1_last", N * PACK, BF16, AT_GROUPED2)
+        regroup_columns(nc.scalar, raw1_last, grouped1_last[:], 0, N // 4)
+        regroup_columns(nc.gpsimd, raw1_last, grouped1_last[:], N // 4, N)
+        quantized.append(w2_first + quantize("w2_last", grouped1_last))
+        a_third = [placed_at(f"a_third{h}", CHUNK, U32, at) for h, at in enumerate((AT_FIRST, AT_TAP2))]
+        b_tap1 = placed_at("b_tap1", V, U32, AT_TAP1)
+        b_third = placed_at("b_third", HALF, U32, AT_THIRD)
         gather_words(1, V, b_tap1[:])
         gather_words(1, 2 * V, b_third[:])
+        gather_words(0, EARLY + CHUNK, a_third[1][:])
 
         def early(first, count):
             pass1 = b_second[:, first - CHUNK : first - CHUNK + count] if first < V else b_tap1[:, first - V : first - V + count]
@@ -179,35 +197,34 @@ def tile_picked_spconv_none_p_kernel(tc, x_words, x_scales, w1, w2, w3, offs, to
         y_first = sbuf("y_first", CHUNK, F32)
         nc.scalar.copy(y_first[:], acc_first[:, 0:CHUNK])
         scatter_on_scalar(0, y_first[:])
-
-        a_third = placed_at("a_third", CHUNK, U32, AT_FIRST)
-        gather_words(0, EARLY, a_third[:])
+        gather_words(0, EARLY, a_third[0][:])
 
         acc0 = bank_at("acc0", HALF, 3)
         multiply(acc0, [(0, HALF, early(HALF, HALF))])
         acc_second = bank_at("acc_second", CHUNK, 0)
         multiply(acc_second, [(0, CHUNK, early(CHUNK, CHUNK))])
         acc1 = bank_at("acc1", HALF, 1)
-        multiply(acc1, [(0, V, early(V, HALF))])
+        acc2 = bank_at("acc2", V, 2)
+        for z in range(PASSES):
+            multiply(acc1, [(0, V, early(V, HALF))], [z])
+            multiply(acc2, [(HALF, V + HALF, early(V + HALF, HALF))], [z])
         y0 = placed_at("y0", V - CHUNK, F32, AT_SECOND)
         nc.scalar.copy(y0[:, CHUNK:], acc0[:])
         nc.scalar.copy(y0[:, 0:CHUNK], acc_second[:])
         scatter_on_scalar(CHUNK, y0[:])
 
-        acc2 = bank_at("acc2", V, 2)
-        multiply(acc2, [(HALF, V + HALF, early(V + HALF, HALF))])
         grouped2 = placed_at("grouped2", PASSES * N * PACK, BF16, AT_GROUPED2)
         for z in range(PASSES):
-            regroup_last_weight(z, raw2[z], grouped2)
+            regroup_columns(nc.gpsimd, raw2[z], grouped2[:, z * N * PACK : (z + 1) * N * PACK], 0, N)
         y1_first = placed_at("y1_first", HALF, F32, AT_RAW2)
         nc.vector.tensor_copy(y1_first[:], acc1[:])
-        quantized.append(quantize(2, grouped2, AT_TAP1))
+        quantized.append(quantize("w3", grouped2, AT_TAP1))
         scatter_on_vector(V, y1_first[:, 0:CHUNK])
         a_last = placed_at("a_last", HALF, U32, AT_GROUPED2)
         gather_words(0, 2 * V + HALF, a_last[:])
         scatter_on_vector(V + CHUNK, y1_first[:, CHUNK:])
 
-        multiply(acc2, [(0, 2 * V, (a_early[:, 2 * V :], b_third[:, 0:CHUNK])), (CHUNK, EARLY, (a_third[:], b_third[:, CHUNK:]))])
+        multiply(acc2, [(CHUNK * h, EARLY + CHUNK * h, (a_third[h][:], b_third[:, CHUNK * h : CHUNK * (h + 1)])) for h in range(2)])
         b_last = placed_at("b_last", HALF, U32, AT_THIRD)
         gather_words(1, 2 * V + HALF, b_last[:])
         y2 = sbuf("y2", V, F32)

@@ -13,6 +13,7 @@ CHUNK = 128
 ROW0 = P - 16 * PASSES
 EARLY = 2 * V
 STORE_COLS = 256
+W3_ON_SCALAR = 48
 BANK = 2048
 AT_RAW2 = 1024
 AT_GROUPED0 = 2560
@@ -20,10 +21,9 @@ AT_LATE_PLANES = 4096
 AT_GROUPED2 = 6144
 AT_SECOND = 8192
 AT_RAW0 = 12288
-AT_TAP1 = AT_RAW0 - 1984
-AT_TAP2 = AT_RAW0 + 64
-AT_FIRST = 0
-AT_THIRD = AT_RAW0 + 1088
+AT_TAP1 = 0
+AT_LATE = AT_RAW0 - 1024
+AT_TAP2 = AT_RAW0 + 1024
 AT_RAW2_FIRST = AT_RAW0 + 2560
 AT_WORDS1 = 18432
 FLOPS = 2 * K * N * S
@@ -169,35 +169,32 @@ def tile_picked_spconv_none_p_kernel(tc, x_words, x_scales, w1, w2, w3, offs, to
             nc.vector.tensor_copy(window(first // V, first % V, y.shape[1]), y)
 
         a_early = sbuf("a_early", EARLY, U32)
-        b_first = placed_at("b_first", CHUNK, U32, AT_FIRST)
+        b_first = sbuf("b_first", CHUNK, U32)
         b_second = placed_at("b_second", V - CHUNK, U32, AT_SECOND)
         gather_words(0, 0, a_early[:])
-        grouped1_first = sbuf("grouped1_first", N * PACK, BF16)
-        regroup_columns(nc.scalar, raw1_first, grouped1_first[:], 0, N)
-        w2_first = quantize("w2_first", grouped1_first)
+        grouped1 = placed_at("grouped1", PASSES * N * PACK, BF16, AT_GROUPED2)
+        regroup_columns(nc.scalar, raw1_first, grouped1[:, 0 : N * PACK], 0, N)
         gather_words(1, 0, b_first[:])
         gather_words(1, CHUNK, b_second[:])
-        grouped1_last = placed_at("grouped1_last", N * PACK, BF16, AT_GROUPED2)
-        regroup_columns(nc.scalar, raw1_last, grouped1_last[:], 0, N // 4)
-        regroup_columns(nc.gpsimd, raw1_last, grouped1_last[:], N // 4, N)
-        quantized.append(w2_first + quantize("w2_last", grouped1_last))
-        a_third = [placed_at(f"a_third{h}", CHUNK, U32, at) for h, at in enumerate((AT_FIRST, AT_TAP2))]
-        b_tap1 = placed_at("b_tap1", V, U32, AT_TAP1)
-        b_third = placed_at("b_third", HALF, U32, AT_THIRD)
+        b_tap1 = placed_at("b_tap1", HALF, U32, AT_TAP1)
         gather_words(1, V, b_tap1[:])
-        gather_words(1, 2 * V, b_third[:])
-        gather_words(0, EARLY + CHUNK, a_third[1][:])
+        regroup_columns(nc.scalar, raw1_last, grouped1[:, N * PACK :], 0, N // 4)
+        regroup_columns(nc.gpsimd, raw1_last, grouped1[:, N * PACK :], N // 4, N)
+        quantized.append(quantize("w2", grouped1))
+        b_late = placed_at("b_late", V, U32, AT_LATE)
+        a_third = placed_at("a_third", HALF, U32, AT_TAP2)
+        gather_words(1, V + HALF, b_late[:])
+        gather_words(0, EARLY, a_third[:])
 
         def early(first, count):
-            pass1 = b_second[:, first - CHUNK : first - CHUNK + count] if first < V else b_tap1[:, first - V : first - V + count]
-            return a_early[:, first : first + count], pass1
+            tile, start = (b_second, CHUNK) if first < V else (b_tap1, V) if first < V + HALF else (b_late, V + HALF)
+            return a_early[:, first : first + count], tile[:, first - start : first - start + count]
 
         acc_first = bank_at("acc_first", 3 * V, 0)
         multiply(acc_first, [(0, 0, (a_early[:, 0:CHUNK], b_first[:]))])
         y_first = sbuf("y_first", CHUNK, F32)
         nc.scalar.copy(y_first[:], acc_first[:, 0:CHUNK])
         scatter_on_scalar(0, y_first[:])
-        gather_words(0, EARLY, a_third[0][:])
 
         acc0 = bank_at("acc0", HALF, 3)
         multiply(acc0, [(0, HALF, early(HALF, HALF))])
@@ -211,11 +208,11 @@ def tile_picked_spconv_none_p_kernel(tc, x_words, x_scales, w1, w2, w3, offs, to
         y0 = placed_at("y0", V - CHUNK, F32, AT_SECOND)
         nc.scalar.copy(y0[:, CHUNK:], acc0[:])
         nc.scalar.copy(y0[:, 0:CHUNK], acc_second[:])
-        scatter_on_scalar(CHUNK, y0[:])
-
         grouped2 = placed_at("grouped2", PASSES * N * PACK, BF16, AT_GROUPED2)
-        for z in range(PASSES):
-            regroup_columns(nc.gpsimd, raw2[z], grouped2[:, z * N * PACK : (z + 1) * N * PACK], 0, N)
+        regroup_columns(nc.scalar, raw2[0], grouped2[:, 0 : N * PACK], 0, W3_ON_SCALAR)
+        scatter_on_scalar(CHUNK, y0[:])
+        regroup_columns(nc.gpsimd, raw2[0], grouped2[:, 0 : N * PACK], W3_ON_SCALAR, N)
+        regroup_columns(nc.gpsimd, raw2[1], grouped2[:, N * PACK :], 0, N)
         y1_first = placed_at("y1_first", HALF, F32, AT_RAW2)
         nc.vector.tensor_copy(y1_first[:], acc1[:])
         quantized.append(quantize("w3", grouped2, AT_TAP1))
@@ -224,8 +221,8 @@ def tile_picked_spconv_none_p_kernel(tc, x_words, x_scales, w1, w2, w3, offs, to
         gather_words(0, 2 * V + HALF, a_last[:])
         scatter_on_vector(V + CHUNK, y1_first[:, CHUNK:])
 
-        multiply(acc2, [(CHUNK * h, EARLY + CHUNK * h, (a_third[h][:], b_third[:, CHUNK * h : CHUNK * (h + 1)])) for h in range(2)])
-        b_last = placed_at("b_last", HALF, U32, AT_THIRD)
+        multiply(acc2, [(0, 2 * V, (a_third[:], b_late[:, HALF:]))])
+        b_last = placed_at("b_last", HALF, U32, AT_TAP2)
         gather_words(1, 2 * V + HALF, b_last[:])
         y2 = sbuf("y2", V, F32)
         nc.scalar.copy(y2[:, 0:HALF], acc2[:, 0:HALF])

@@ -112,10 +112,12 @@ def tile_picked_spconv_none_p_kernel(tc, x_words, x_scales, w1, w2, w3, offs, to
         load_words(0)
         load_pass(1, 0, raw1_first)
 
-        nc.vector.memset(zero[:], 0.0)
+        zeros = (zero, sbuf("zero_last", 1, F32))
+        for source in zeros:
+            nc.vector.memset(source[:], 0.0)
         nc.vector.memset(placed[1][:], 0.0)
-        for d in (0, 2):
-            nc.scalar.activation(placed[d][:], zero[:].to_broadcast([P, U]), COPY)
+        for d, source in zip((0, 2), zeros):
+            nc.scalar.activation(placed[d][:], source[:].to_broadcast([P, U]), COPY)
 
         def gather_scales(name, first, count):
             picked = sbuf(name, count, U8)
@@ -171,7 +173,8 @@ def tile_picked_spconv_none_p_kernel(tc, x_words, x_scales, w1, w2, w3, offs, to
         a_early = sbuf("a_early", EARLY, U32)
         b_first = sbuf("b_first", CHUNK, U32)
         b_second = placed_at("b_second", V - CHUNK, U32, AT_SECOND)
-        gather_words(0, 0, a_early[:])
+        gather_words(0, 0, a_early[:, 0:V])
+        gather_words(0, V, a_early[:, V:])
         grouped1 = placed_at("grouped1", PASSES * N * PACK, BF16, AT_GROUPED2)
         regroup_columns(nc.scalar, raw1_first, grouped1[:, 0 : N * PACK], 0, N)
         gather_words(1, 0, b_first[:])

@@ -13,7 +13,7 @@ CHUNK = 128
 ROW0 = P - 16 * PASSES
 EARLY = 2 * V
 STORE_COLS = 256
-W3_ON_SCALAR = 48
+W3_ON_SCALAR = 64
 BANK = 2048
 AT_RAW2 = 1024
 AT_GROUPED0 = 2560
@@ -216,13 +216,15 @@ def tile_picked_spconv_none_p_kernel(tc, x_words, x_scales, w1, w2, w3, offs, to
         scatter_on_scalar(CHUNK, y0[:])
         regroup_columns(nc.gpsimd, raw2[0], grouped2[:, 0 : N * PACK], W3_ON_SCALAR, N)
         regroup_columns(nc.gpsimd, raw2[1], grouped2[:, N * PACK :], 0, N)
-        y1_first = placed_at("y1_first", HALF, F32, AT_RAW2)
-        nc.vector.tensor_copy(y1_first[:], acc1[:])
+        y1_second = sbuf("y1_second", CHUNK, F32)
+        nc.vector.tensor_copy(y1_second[:], acc1[:, CHUNK:])
+        y1_first = placed_at("y1_first", CHUNK, F32, AT_RAW2)
+        nc.vector.tensor_copy(y1_first[:], acc1[:, 0:CHUNK])
         quantized.append(quantize("w3", grouped2, AT_TAP1))
-        scatter_on_vector(V, y1_first[:, 0:CHUNK])
+        scatter_on_vector(V, y1_first[:])
         a_last = placed_at("a_last", HALF, U32, AT_GROUPED2)
         gather_words(0, 2 * V + HALF, a_last[:])
-        scatter_on_vector(V + CHUNK, y1_first[:, CHUNK:])
+        scatter_on_vector(V + CHUNK, y1_second[:])
 
         multiply(acc2, [(0, 2 * V, (a_third[:], b_late[:, HALF:]))])
         b_last = placed_at("b_last", HALF, U32, AT_TAP2)

@@ -173,17 +173,18 @@ def tile_picked_spconv_none_p_kernel(tc, x_words, x_scales, w1, w2, w3, offs, to
         a_early = sbuf("a_early", EARLY, U32)
         b_first = sbuf("b_first", CHUNK, U32)
         b_second = placed_at("b_second", V - CHUNK, U32, AT_SECOND)
-        gather_words(0, 0, a_early[:, 0:V])
-        gather_words(0, V, a_early[:, V:])
-        grouped1 = placed_at("grouped1", PASSES * N * PACK, BF16, AT_GROUPED2)
-        regroup_columns(nc.scalar, raw1_first, grouped1[:, 0 : N * PACK], 0, N)
+        gather_words(0, 0, a_early[:])
+        grouped1_first = sbuf("grouped1_first", N * PACK, BF16)
+        regroup_columns(nc.scalar, raw1_first, grouped1_first[:], 0, N)
+        w2_first = quantize("w2_first", grouped1_first)
         gather_words(1, 0, b_first[:])
         gather_words(1, CHUNK, b_second[:])
         b_tap1 = placed_at("b_tap1", HALF, U32, AT_TAP1)
         gather_words(1, V, b_tap1[:])
-        regroup_columns(nc.scalar, raw1_last, grouped1[:, N * PACK :], 0, N // 4)
-        regroup_columns(nc.gpsimd, raw1_last, grouped1[:, N * PACK :], N // 4, N)
-        quantized.append(quantize("w2", grouped1))
+        grouped1_last = placed_at("grouped1_last", N * PACK, BF16, AT_GROUPED2)
+        regroup_columns(nc.scalar, raw1_last, grouped1_last[:], 0, N // 4)
+        regroup_columns(nc.gpsimd, raw1_last, grouped1_last[:], N // 4, N)
+        quantized.append(w2_first + quantize("w2_last", grouped1_last))
         b_late = placed_at("b_late", V, U32, AT_LATE)
         a_third = placed_at("a_third", HALF, U32, AT_TAP2)
         gather_words(1, V + HALF, b_late[:])

@@ -13,7 +13,7 @@ CHUNK = 128
 ROW0 = P - 16 * PASSES
 EARLY = 2 * V
 STORE_COLS = 256
-W3_ON_SCALAR = 64
+W3_ON_SCALAR = 48
 BANK = 2048
 AT_RAW2 = 1024
 AT_GROUPED0 = 2560
@@ -107,8 +107,7 @@ def tile_picked_spconv_none_p_kernel(tc, x_words, x_scales, w1, w2, w3, offs, to
         nc.sync.dma_start(picks[:], offs)
         nc.vector.memset(scale_table[0:ROW0, :].bitcast(I32), 0)
         load_weight(0, raw0)
-        for tile, dram in zip(maps, (to1, to2, to3)):
-            nc.sync.dma_start(tile[:], dram)
+        nc.sync.dma_start(maps[0][:], to1)
         load_words(0)
         load_pass(1, 0, raw1_first)
 
@@ -142,6 +141,8 @@ def tile_picked_spconv_none_p_kernel(tc, x_words, x_scales, w1, w2, w3, offs, to
         late_planes = placed_at("late_planes", PASSES * (S - V), U8, AT_LATE_PLANES)
         move_rows(late_rows, late_planes)
         load_pass(2, 1, raw2[1])
+        nc.sync.dma_start(maps[1][:], to2)
+        nc.sync.dma_start(maps[2][:], to3)
 
         def x_scale(z, first, count):
             if first < V:

from contextlib import ExitStack

import concourse.mybir as mybir

K, T, S, V, N, U = 1024, 2048, 1536, 512, 128, 1024
TAPS = 3
P = 128
PACK = 4
QUADS = 4
PASSES = K // (P * PACK)
HALF = V // 2
CHUNK = 128
ROW0 = P - 16 * PASSES
EARLY = 2 * V
STORE_COLS = 256
W3_ON_SCALAR = 48
BANK = 2048
AT_RAW2 = 1024
AT_GROUPED0 = 2560
AT_LATE_PLANES = 4096
AT_GROUPED2 = 6144
AT_SECOND = 8192
AT_RAW0 = 12288
AT_TAP1 = 0
AT_LATE = AT_RAW0 - 1024
AT_TAP2 = AT_RAW0 + 1024
AT_RAW2_FIRST = AT_RAW0 + 2560
AT_WORDS1 = 18432
FLOPS = 2 * K * N * S

F32 = mybir.dt.float32
BF16 = mybir.dt.bfloat16
I32 = mybir.dt.int32
U32 = mybir.dt.uint32
U16 = mybir.dt.uint16
U8 = mybir.dt.uint8
FP8X4 = mybir.dt.float8_e4m3fn_x4
ADD = mybir.AluOpType.add
MULT = mybir.AluOpType.mult
COPY = mybir.ActivationFunctionType.Copy


def tile_picked_spconv_none_p_kernel(tc, x_words, x_scales, w1, w2, w3, offs, to1, to2, to3, out):
    nc = tc.nc
    weights = (w1, w2, w3)
    with ExitStack() as ctx:
        keep = ctx.enter_context(tc.tile_pool(name="keep", bufs=1))
        reuse = ctx.enter_context(tc.tile_pool(name="reuse", bufs=1))
        psum = ctx.enter_context(tc.psum_pool(name="psum", bufs=1))

        def sbuf(name, cols, dtype):
            return keep.tile([P, cols], dtype, name=name, align_bytes=64)

        def placed_at(name, cols, dtype, offset):
            return reuse.tile([P, cols], dtype, name=name, align_bytes=64, offset=offset)

        def bank_at(name, cols, bank):
            return psum.tile([P, cols], F32, name=name, offset=bank * BANK)

        picks = keep.tile([P, S // 16], U16, name="picks")
        maps = [keep.tile([P, V // 16], U16, name=f"map{d}") for d in range(TAPS)]
        scale_table = sbuf("scale_table", T, U8)
        zero = placed_at("zero", 1, F32, AT_WORDS1)
        word_tables = [sbuf("word_table0", T, I32), placed_at("word_table1", T, I32, AT_WORDS1)]
        placed = [sbuf(f"placed{d}", U, F32) for d in range(TAPS)]

        def load_words(z):
            nc.sync.dma_start(word_tables[z][:], x_words[z].rearrange("p c r -> p (c r)").bitcast(I32))

        def load_weight(d, raw):
            nc.sync.dma_start(raw[:].rearrange("p (z r) -> p z r", z=PASSES), weights[d].rearrange("(z p j) m -> p z (j m)", z=PASSES, j=PACK))

        def regroup(d, raw, grouped):
            src = raw[:].rearrange("p (z j m) -> p z m j", z=PASSES, j=PACK)
            dst = grouped[:].rearrange("p (z m j) -> p z m j", z=PASSES, j=PACK)
            nc.scalar.copy(dst, src)
            return grouped

        def load_pass(d, z, raw):
            nc.sync.dma_start(raw[:], weights[d][z * P * PACK : (z + 1) * P * PACK, :].rearrange("(p j) m -> p (j m)", j=PACK))

        def regroup_columns(engine, raw, grouped, lo, hi):
            src = raw[:].rearrange("p (j m) -> p m j", j=PACK)[:, lo:hi, :]
            dst = grouped.rearrange("p (m j) -> p m j", j=PACK)[:, lo:hi, :]
            if engine is nc.scalar:
                nc.scalar.copy(dst, src)
            else:
                nc.gpsimd.tensor_scalar(dst, src, 1.0, 0.0, MULT, ADD)

        def quantize(name, grouped, at=None):
            cols = grouped.shape[1] // PACK
            codes = sbuf(f"codes_{name}", cols, U32) if at is None else placed_at(f"codes_{name}", cols, U32, at)
            scale = sbuf(f"scale_{name}", cols, U8)
            nc.vector.quantize_mx(out=codes[:].bitcast(FP8X4), scales=scale[:], in_=grouped[:])
            return [(codes[:, c : c + N], scale[:, c : c + N]) for c in range(0, cols, N)]

        def gather_words(z, first, piece):
            count = piece.shape[1]
            nc.vector.tensor_copy(piece, word_tables[z][:].bitcast(U32).indirect(picks[:, first // 16 : (first + count) // 16]))

        def window(d, first, count):
            return placed[d][:].indirect(maps[d][:, first // 16 : (first + count) // 16])

        raw0 = placed_at("raw0", PASSES * PACK * N, F32, AT_RAW0)
        raw1_first = sbuf("raw1_first", PACK * N, F32)
        nc.sync.dma_start(scale_table[ROW0:P, :].bitcast(I32), x_scales.bitcast(I32).rearrange("z r c -> r z c"))
        nc.sync.dma_start(picks[:], offs)
        nc.vector.memset(scale_table[0:ROW0, :].bitcast(I32), 0)
        load_weight(0, raw0)
        nc.sync.dma_start(maps[0][:], to1)
        load_words(0)
        load_pass(1, 0, raw1_first)

        zeros = (zero, sbuf("zero_last", 1, F32))
        for source in zeros:
            nc.vector.memset(source[:], 0.0)
        nc.vector.memset(placed[1][:], 0.0)
        for d, source in zip((0, 2), zeros):
            nc.scalar.activation(placed[d][:], source[:].to_broadcast([P, U]), COPY)

        def gather_scales(name, first, count):
            picked = sbuf(name, count, U8)
            nc.vector.tensor_copy(picked[:], scale_table[:].indirect(picks[:, first // 16 : (first + count) // 16]))
            return picked

        def move_rows(picked, planes):
            for q in range(QUADS):
                rows = planes[32 * q : 32 * q + 4, :].bitcast(I32).rearrange("p (z c) -> p z c", z=PASSES)
                nc.sync.dma_start(rows, picked[ROW0 + 8 * q : ROW0 + 8 * (q + 1), :].bitcast(I32))

        first_planes = sbuf("first_planes", PASSES * V, U8)
        move_rows(gather_scales("first_rows", 0, V), first_planes)
        load_words(1)
        late_rows = gather_scales("late_rows", V, S - V)

        quantized = [quantize("w1", regroup(0, raw0, placed_at("grouped0", PASSES * N * PACK, BF16, AT_GROUPED0)))]
        raw1_last = placed_at("raw1_last", PACK * N, F32, AT_RAW0)
        load_pass(1, 1, raw1_last)
        raw2 = [placed_at(f"raw2_{z}", PACK * N, F32, at) for z, at in enumerate((AT_RAW2_FIRST, AT_RAW2))]
        load_pass(2, 0, raw2[0])
        late_planes = placed_at("late_planes", PASSES * (S - V), U8, AT_LATE_PLANES)
        move_rows(late_rows, late_planes)
        load_pass(2, 1, raw2[1])
        nc.sync.dma_start(maps[1][:], to2)
        nc.sync.dma_start(maps[2][:], to3)

        def x_scale(z, first, count):
            if first < V:
                return first_planes[:, z * V + first : z * V + first + count]
            at = z * (S - V) + first - V
            return late_planes[:, at : at + count]

        def multiply(acc, spans, passes=range(PASSES)):
            steps = [(z, span) for z in passes for span in spans]
            for z, (at, first, moving) in steps:
                codes, scale = quantized[first // V][z]
                count = moving[0].shape[1]
                nc.tensor.matmul_mx(
                    out=acc[:, at : at + count],
                    lhsT=codes.bitcast(FP8X4),
                    lhsT_scale=scale,
                    rhs=moving[z].bitcast(FP8X4),
                    rhs_scale=x_scale(z, first, count),
                    start=((z, at) == (0, spans[0][0])),
                    stop=((z, at) == (PASSES - 1, spans[-1][0])),
                )

        def scatter_on_scalar(first, y):
            nc.scalar.activation(window(first // V, first % V, y.shape[1]), y, COPY)

        def scatter_on_vector(first, y):
            nc.vector.tensor_copy(window(first // V, first % V, y.shape[1]), y)

        a_early = sbuf("a_early", EARLY, U32)
        b_first = sbuf("b_first", CHUNK, U32)
        b_second = placed_at("b_second", V - CHUNK, U32, AT_SECOND)
        gather_words(0, 0, a_early[:])
        grouped1_first = sbuf("grouped1_first", N * PACK, BF16)
        regroup_columns(nc.scalar, raw1_first, grouped1_first[:], 0, N)
        w2_first = quantize("w2_first", grouped1_first)
        gather_words(1, 0, b_first[:])
        gather_words(1, CHUNK, b_second[:])
        b_tap1 = placed_at("b_tap1", HALF, U32, AT_TAP1)
        gather_words(1, V, b_tap1[:])
        grouped1_last = placed_at("grouped1_last", N * PACK, BF16, AT_GROUPED2)
        regroup_columns(nc.scalar, raw1_last, grouped1_last[:], 0, N // 4)
        regroup_columns(nc.gpsimd, raw1_last, grouped1_last[:], N // 4, N)
        quantized.append(w2_first + quantize("w2_last", grouped1_last))
        b_late = placed_at("b_late", V, U32, AT_LATE)
        a_third = placed_at("a_third", HALF, U32, AT_TAP2)
        gather_words(1, V + HALF, b_late[:])
        gather_words(0, EARLY, a_third[:])

        def early(first, count):
            tile, start = (b_second, CHUNK) if first < V else (b_tap1, V) if first < V + HALF else (b_late, V + HALF)
            return a_early[:, first : first + count], tile[:, first - start : first - start + count]

        acc_first = bank_at("acc_first", 3 * V, 0)
        multiply(acc_first, [(0, 0, (a_early[:, 0:CHUNK], b_first[:]))])
        y_first = sbuf("y_first", CHUNK, F32)
        nc.scalar.copy(y_first[:], acc_first[:, 0:CHUNK])
        scatter_on_scalar(0, y_first[:])

        acc0 = bank_at("acc0", HALF, 3)
        multiply(acc0, [(0, HALF, early(HALF, HALF))])
        acc_second = bank_at("acc_second", CHUNK, 0)
        multiply(acc_second, [(0, CHUNK, early(CHUNK, CHUNK))])
        acc1 = bank_at("acc1", HALF, 1)
        acc2 = bank_at("acc2", V, 2)
        for z in range(PASSES):
            multiply(acc1, [(0, V, early(V, HALF))], [z])
            multiply(acc2, [(HALF, V + HALF, early(V + HALF, HALF))], [z])
        y0 = placed_at("y0", V - CHUNK, F32, AT_SECOND)
        nc.scalar.copy(y0[:, CHUNK:], acc0[:])
        nc.scalar.copy(y0[:, 0:CHUNK], acc_second[:])
        grouped2 = placed_at("grouped2", PASSES * N * PACK, BF16, AT_GROUPED2)
        regroup_columns(nc.scalar, raw2[0], grouped2[:, 0 : N * PACK], 0, W3_ON_SCALAR)
        scatter_on_scalar(CHUNK, y0[:])
        regroup_columns(nc.gpsimd, raw2[0], grouped2[:, 0 : N * PACK], W3_ON_SCALAR, N)
        regroup_columns(nc.gpsimd, raw2[1], grouped2[:, N * PACK :], 0, N)
        y1_second = sbuf("y1_second", CHUNK, F32)
        nc.vector.tensor_copy(y1_second[:], acc1[:, CHUNK:])
        y1_first = placed_at("y1_first", CHUNK, F32, AT_RAW2)
        nc.vector.tensor_copy(y1_first[:], acc1[:, 0:CHUNK])
        quantized.append(quantize("w3", grouped2, AT_TAP1))
        scatter_on_vector(V, y1_first[:])
        a_last = placed_at("a_last", HALF, U32, AT_GROUPED2)
        gather_words(0, 2 * V + HALF, a_last[:])
        scatter_on_vector(V + CHUNK, y1_second[:])

        multiply(acc2, [(0, 2 * V, (a_third[:], b_late[:, HALF:]))])
        b_last = placed_at("b_last", HALF, U32, AT_TAP2)
        gather_words(1, 2 * V + HALF, b_last[:])
        y2 = sbuf("y2", V, F32)
        nc.scalar.copy(y2[:, 0:HALF], acc2[:, 0:HALF])
        y1_last = sbuf("y1_last", HALF, F32)
        nc.scalar.copy(y1_last[:], acc2[:, HALF:])
        scatter_on_scalar(2 * V, y2[:, 0:HALF])
        scatter_on_vector(V + HALF, y1_last[:])
        acc_last = bank_at("acc_last", HALF, 2)
        multiply(acc_last, [(0, 2 * V + HALF, (a_last[:], b_last[:]))])
        nc.scalar.copy(y2[:, HALF:], acc_last[:])
        scatter_on_scalar(2 * V + HALF, y2[:, HALF:])

        pair = sbuf("pair", U, F32)
        for half in (slice(0, U // 2), slice(U // 2, U)):
            nc.vector.tensor_tensor(pair[:, half], placed[0][:, half], placed[1][:, half], ADD)
        for c in range(U // STORE_COLS):
            cols = slice(c * STORE_COLS, (c + 1) * STORE_COLS)
            total = sbuf(f"total{c}", STORE_COLS, F32)
            nc.vector.tensor_tensor(total[:], pair[:, cols], placed[2][:, cols], ADD)
            nc.sync.dma_start(out[:, cols], total[:])
